import numpy as np
import ml_dtypes


def mxq(x, axis, fmt="e4m3"):
    dtype, down = {"e4m3": (ml_dtypes.float8_e4m3fn, 7), "e5m2": (ml_dtypes.float8_e5m2, 14)}[fmt]
    v = np.moveaxis(np.asarray(x, np.float32).astype(ml_dtypes.bfloat16).astype(np.float64), axis, -1)
    blocks = v.reshape(v.shape[:-1] + (-1, 32))
    amax = np.abs(blocks).max(-1, keepdims=True)
    byte = np.maximum(np.where(amax > 0, np.frexp(amax)[1] - 1 + 127, 0) - down, 1)
    scale = np.exp2(byte - 127.0)
    codes = (blocks / scale).astype(np.float32).astype(dtype).astype(np.float64)
    return np.moveaxis((codes * scale).reshape(v.shape), -1, axis)


WIDE = False


def mx_kscale(k):
    if not WIDE:
        return np.ones(k)
    levels = np.array([10, -10, 5, -5, 0])
    if k % 512:
        return np.exp2(np.random.permutation(np.resize(levels, k // 32))).repeat(32)
    a = np.empty((k // 512, 16))
    for p in range(k // 512):
        a[p, :8] = np.random.permutation(np.resize(levels, 8))
        for g in range(8):
            far = levels[np.abs(levels - a[p, g]) >= 10]
            a[p, g + 8] = far[np.random.randint(len(far))]
    return np.exp2(a.ravel()).repeat(32)


def f64(x):
    return np.asarray(x).astype(np.float64)


def striped(idx):
    return np.tile(idx.reshape(-1, 16).T, (8, 1)).astype(np.uint16)


def unstriped(offs):
    return offs[:16].T.reshape(-1).astype(np.int64)


def pack_weight(w):
    k, n = w.shape
    w = f64(np.asarray(w, np.float32).astype(ml_dtypes.bfloat16)).reshape(k // 32, 32, n)
    amax = np.abs(w).max(1)
    byte = np.clip(np.where(amax > 0, np.frexp(amax)[1] - 1 + 127 - 7, 1), 1, 254)
    scaled = (w * np.exp2(127.0 - byte)[:, None, :]).reshape(k, n).astype(np.float32)
    words = np.ascontiguousarray(scaled.reshape(k // 512, 128, 4, n).transpose(0, 1, 3, 2)).astype(ml_dtypes.float8_e4m3fn).view(np.uint8)
    return words, np.ascontiguousarray(byte.astype(np.uint8).reshape(k // 512, 16, n))


def unpack_weight(words, scales):
    g, p, n, _ = words.shape
    vals = np.ascontiguousarray(words).view(ml_dtypes.float8_e4m3fn).astype(np.float64) * np.repeat(np.exp2(scales.astype(np.float64) - 127.0), 8, axis=1)[..., None]
    return vals.transpose(0, 1, 3, 2).reshape(g * 512, n)


def planes(y):
    n, m = y.shape
    v = y.astype(np.float32).astype(ml_dtypes.bfloat16).astype(np.float64).reshape(n // 32, 32, m)
    top = np.abs(v).max(1)
    byte = np.clip(np.where(top > 0, np.frexp(top)[1] - 1 + 127 - 7, 1), 1, 254)
    codes = (v * np.exp2(127.0 - byte)[:, None, :]).reshape(n, m).astype(np.float32).astype(ml_dtypes.float8_e4m3fn).view(np.uint8)
    words = codes.reshape(n // 512, 128, 4, m).transpose(0, 1, 3, 2)
    return np.ascontiguousarray(words), np.ascontiguousarray(byte.astype(np.uint8).reshape(n // 512, 16, m))


K, T, S, D, V, H, N, U = 512, 4096, 1024, 3, 512, 512, 512, 256
P = 2 ** 7


def setup_inputs():
    n = np.random.standard_normal
    s = mx_kscale(K)[:, None]
    u = mx_kscale(H)
    near = np.random.permutation(S)
    next_ = np.random.permutation(V)
    packed_xT = pack_weight(n((K, T)) * s)
    packed_w2 = pack_weight(n((H, N)) / np.sqrt(H) / u[:, None])
    return {
        "x_words": packed_xT[0],
        "x_scales": packed_xT[1],
        "w1": (n((K, H)) / np.sqrt(K) / s * u).astype(np.float32),
        "w2_words": packed_w2[0],
        "w2_scales": packed_w2[1],
        "gate": (np.tile(np.random.uniform(0.2, 1.0, (D, 1, V)) / np.sqrt(D), (1, P, 1))).astype(np.float32),
        "gate2": (np.tile(np.random.uniform(0.2, 1.0, (D, 1, U)) / np.sqrt(D), (1, P, 1))).astype(np.float32),
        "offs": striped(np.random.permutation(T)[:S]),
        "cen": striped(np.random.permutation(S)[:V]),
        "pos1": striped(near[:V]),
        "pos2": striped(near[V:]),
        "pos3": striped(np.random.permutation(S)[:V]),
        "nxt1": striped(next_[:U]),
        "nxt2": striped(next_[U:]),
        "nxt3": striped(np.random.permutation(V)[:U]),
        "root": striped(np.random.permutation(S)[:U]),
    }


def reference(x_words, x_scales, w1, w2_words, w2_scales, gate, gate2, offs, cen, pos1, pos2, pos3, nxt1, nxt2, nxt3, root):
    xq = unpack_weight(x_words, x_scales)[:, unstriped(offs)]
    h = mxq(f64(w1), 0, "e4m3").T @ xq
    y = unpack_weight(w2_words, w2_scales).T @ mxq(h, 0, "e4m3")
    z = 0.8 * (y[:, unstriped(pos1)] * f64(gate)[0, :1] + y[:, unstriped(pos2)] * f64(gate)[1, :1] + y[:, unstriped(pos3)] * f64(gate)[2, :1]) + 0.2 * y[:, unstriped(cen)]
    out_0 = 0.8 * (z[:, unstriped(nxt1)] * f64(gate2)[0, :1] + z[:, unstriped(nxt2)] * f64(gate2)[1, :1] + z[:, unstriped(nxt3)] * f64(gate2)[2, :1]) + 0.2 * y[:, unstriped(root)]
    return (out_0,) + planes(out_0)

@@ -1,0 +1,256 @@
+from contextlib import ExitStack
+
+import concourse.mybir as mybir
+from concourse.masks import make_identity
+
+K, T, S, D, V, H, N, U = 512, 4096, 1024, 3, 512, 512, 512, 256
+FLOPS = 2 * K * H * S + 2 * H * N * S
+
+F32 = mybir.dt.float32
+BF16 = mybir.dt.bfloat16
+I32 = mybir.dt.int32
+U32 = mybir.dt.uint32
+U16 = mybir.dt.uint16
+U8 = mybir.dt.uint8
+FP8X4 = mybir.dt.float8_e4m3fn_x4
+MULT = mybir.AluOpType.mult
+ADD = mybir.AluOpType.add
+COPY = mybir.ActivationFunctionType.Copy
+
+P = 128
+PACK = 4
+HALF = S // 2
+CHUNK = 128
+PIECE = 256
+VECTOR_CHUNKS = (5, 7)
+VECTOR_PIECES = (3,)
+
+
+def tile_picked_zappnp_none_po_kernel(
+    tc, x_words, x_scales, w1, w2_words, w2_scales, gate, gate2,
+    offs, cen, pos1, pos2, pos3, nxt1, nxt2, nxt3, root, out_0, out_1, out_2,
+):
+    nc = tc.nc
+    with ExitStack() as ctx:
+        lists = ctx.enter_context(tc.tile_pool(name="lists", bufs=1))
+        keep = ctx.enter_context(tc.tile_pool(name="keep", bufs=1))
+        ring = ctx.enter_context(tc.tile_pool(name="ring", bufs=2))
+        psum = ctx.enter_context(tc.psum_pool(name="psum", bufs=4))
+
+        def load_list(name, source):
+            tile = lists.tile(list(source.shape), U16, name=name)
+            nc.sync.dma_start(tile[:], source)
+            return tile
+
+        def load_scale_rows(tile, source):
+            nc.vector.memset(tile[:].bitcast(I32), 0)
+            for q in range(4):
+                nc.gpsimd.dma_start(
+                    out=tile[32 * q : 32 * q + 4, :].bitcast(I32),
+                    in_=source[0, 4 * q : 4 * q + 4, :].bitcast(I32),
+                )
+
+        x_scale_table = keep.tile([P, T], U8, tag="x_bytes", align_bytes=64)
+        load_scale_rows(x_scale_table, x_scales)
+        w2_scale_rows = keep.tile([P, N], U8, align_bytes=64)
+        load_scale_rows(w2_scale_rows, w2_scales)
+
+        w1_raw = keep.tile([P, PACK, H], F32, align_bytes=64)
+        nc.sync.dma_start(out=w1_raw[:], in_=w1.rearrange("(p j) c -> p j c", j=PACK))
+        offs_t = load_list("offs_t", offs)
+        x_word_table = keep.tile([P, T], U32, align_bytes=64)
+        nc.sync.dma_start(
+            out=x_word_table[:].bitcast(I32),
+            in_=x_words[0].rearrange("p c r -> p (c r)").bitcast(I32),
+        )
+        w2_raw = keep.tile([P, N], I32, align_bytes=64)
+        nc.sync.dma_start(out=w2_raw[:], in_=w2_words[0].rearrange("p c r -> p (c r)").bitcast(I32))
+        gate_t = keep.tile([P, D, V], F32, align_bytes=64)
+        nc.sync.dma_start(out=gate_t[:], in_=gate.rearrange("d p v -> p d v"))
+        pos_t = [load_list("pos%d_t" % d, src) for d, src in enumerate((pos1, pos2, pos3))]
+        cen_t = load_list("cen_t", cen)
+        nxt_t = [load_list("nxt%d_t" % d, src) for d, src in enumerate((nxt1, nxt2, nxt3))]
+        root_t = load_list("root_t", root)
+        gate2_raw = keep.tile([P, D, U], F32, align_bytes=64)
+        nc.sync.dma_start(out=gate2_raw[:], in_=gate2.rearrange("d p x -> p d x"))
+
+        identity = keep.tile([P, P], F32, align_bytes=64)
+        make_identity(nc, identity[:])
+
+        w1_codes = keep.tile([P, H], U32, align_bytes=64)
+        w1_sc = keep.tile([P, H], U8, align_bytes=64)
+        w1_view = w1_raw[:].rearrange("p j (m t) -> p m t j", t=PACK)
+        for u in range(2):
+            w1_bf = keep.tile([P, 2, P, PACK], BF16, name="w1_bf%d" % u, align_bytes=64)
+            dst = w1_bf[:].rearrange("p t m j -> p m t j")
+            src = w1_view[:, :, 2 * u : 2 * u + 2, :]
+            if u == 0:
+                nc.vector.tensor_copy(out=dst, in_=src)
+            else:
+                nc.scalar.activation(out=dst, in_=src, func=COPY)
+            cols = slice(2 * P * u, 2 * P * (u + 1))
+            nc.vector.quantize_mx(
+                out=w1_codes[:, cols].bitcast(FP8X4),
+                scales=w1_sc[:, cols],
+                in_=w1_bf[:].rearrange("p t m j -> p (t m j)"),
+            )
+
+        x_sc = keep.tile([P, S], U8, align_bytes=64)
+        nc.vector.tensor_copy(x_sc[:], x_scale_table[:].indirect(offs_t[:]))
+        x_codes = keep.tile([P, S], U32, tag="x_bytes", align_bytes=64)
+        w2_sc = keep.tile([P, PACK, P], U8, align_bytes=64)
+        nc.vector.tensor_copy(
+            out=w2_sc[:].rearrange("p t m -> p m t"),
+            in_=w2_scale_rows[:].rearrange("p (m t) -> p m t", t=PACK),
+        )
+        for u in range(2):
+            nc.vector.tensor_copy(
+                x_codes[:, u * HALF : (u + 1) * HALF],
+                x_word_table[:].indirect(offs_t[:, u * HALF // 16 : (u + 1) * HALF // 16]),
+            )
+        w2_codes = keep.tile([P, PACK, P], I32, align_bytes=64)
+        nc.vector.tensor_copy(
+            out=w2_codes[:].rearrange("p t m -> p m t"),
+            in_=w2_raw[:].rearrange("p (m t) -> p m t", t=PACK),
+        )
+
+        h_codes = keep.tile([P, S], U32, align_bytes=64)
+        h_sc = keep.tile([P, S], U8, align_bytes=64)
+        y = [keep.tile([P, S], F32, name="y%d" % t, align_bytes=64) for t in range(PACK)]
+
+        def second_layer(t, cols, on_vector):
+            bank = psum.tile([P, cols.stop - cols.start], F32, name="y_bank", tag="b")
+            nc.tensor.matmul_mx(
+                out=bank[:],
+                lhsT=w2_codes[:, t, :].bitcast(FP8X4),
+                lhsT_scale=w2_sc[:, t, :],
+                rhs=h_codes[:, cols].bitcast(FP8X4),
+                rhs_scale=h_sc[:, cols],
+                start=True,
+                stop=True,
+            )
+            if on_vector:
+                nc.vector.tensor_scalar_mul(y[t][:, cols], bank[:], 0.2)
+            else:
+                nc.scalar.activation(out=y[t][:, cols], in_=bank[:], func=COPY, scale=0.2)
+
+        for piece in range(S // PIECE):
+            h_bf = keep.tile([P, PIECE, PACK], BF16, name="h_bf", tag="h_bf%d" % piece, align_bytes=64)
+            for c in range(PIECE // CHUNK):
+                chunk = piece * (PIECE // CHUNK) + c
+                cols = slice(chunk * CHUNK, (chunk + 1) * CHUNK)
+                bank = psum.tile([P, PACK, CHUNK], F32, name="h_bank", tag="a")
+                for t in range(PACK):
+                    nc.tensor.matmul_mx(
+                        out=bank[:, t, :],
+                        lhsT=w1_codes[:, t * P : (t + 1) * P].bitcast(FP8X4),
+                        lhsT_scale=w1_sc[:, t * P : (t + 1) * P],
+                        rhs=x_codes[:, cols].bitcast(FP8X4),
+                        rhs_scale=x_sc[:, cols],
+                        start=True,
+                        stop=True,
+                    )
+                dst = h_bf[:, c * CHUNK : (c + 1) * CHUNK, :]
+                src = bank[:].rearrange("p t n -> p n t")
+                if chunk in VECTOR_CHUNKS:
+                    nc.vector.tensor_copy(out=dst, in_=src)
+                else:
+                    nc.scalar.copy(out=dst, in_=src)
+            cols = slice(piece * PIECE, (piece + 1) * PIECE)
+            nc.vector.quantize_mx(
+                out=h_codes[:, cols].bitcast(FP8X4),
+                scales=h_sc[:, cols],
+                in_=h_bf[:].rearrange("p n t -> p (n t)"),
+            )
+            second_layer(0, cols, piece in VECTOR_PIECES)
+        for t in range(1, PACK):
+            for u in range(2):
+                second_layer(t, slice(u * HALF, (u + 1) * HALF), False)
+
+        gate2_t = keep.tile([P, D, U], F32, name="gate2_t", tag="h_bf%d" % (S // PIECE - 1), align_bytes=64)
+        nc.scalar.activation(out=gate2_t[:], in_=gate2_raw[:], func=COPY, scale=0.8)
+
+        def sum_on_tensor(terms, width, scale, dst):
+            turned = psum.tile([P, width], F32, name="turned", tag="a")
+            for b in range(width // P):
+                cols = slice(b * P, (b + 1) * P)
+                for i, term in enumerate(terms):
+                    nc.tensor.matmul(
+                        turned[:, cols], term[:, cols], identity[:],
+                        start=(i == 0), stop=(i == len(terms) - 1), is_transpose=True,
+                    )
+            turned_sb = ring.tile([P, width], F32, name="turned_sb", align_bytes=64)
+            nc.scalar.activation(out=turned_sb[:], in_=turned[:], func=COPY, scale=scale)
+            back = psum.tile([P, width], F32, name="back", tag="b")
+            for b in range(width // P):
+                cols = slice(b * P, (b + 1) * P)
+                nc.tensor.transpose(back[:, cols], turned_sb[:, cols], identity[:])
+            nc.scalar.copy(out=dst, in_=back[:])
+
+        z = [keep.tile([P, V], F32, name="z%d" % t, align_bytes=64) for t in range(PACK)]
+        mixed = [keep.tile([P, V], F32, name="mixed%d" % t, align_bytes=64) for t in range(PACK)]
+        result = keep.tile([P, PACK, U], F32, align_bytes=64)
+        out_rows = out_0.rearrange("(p t) x -> p t x", t=PACK)
+
+        def neighbours_1(t):
+            terms = []
+            for d in range(D):
+                term = keep.tile([P, V], F32, name="near%d_%d" % (t, d), align_bytes=64)
+                nc.vector.tensor_tensor(term[:], y[t][:].indirect(pos_t[d][:]), gate_t[:, d, :], MULT)
+                terms.append(term)
+            sum_on_tensor(terms, V, 4.0, mixed[t][:])
+
+        def restart_1(t):
+            nc.vector.tensor_tensor(z[t][:], y[t][:].indirect(cen_t[:]), mixed[t][:], ADD)
+
+        def step_2(t):
+            terms = []
+            for d in range(D):
+                term = keep.tile([P, U], F32, name="far%d_%d" % (t, d), align_bytes=64)
+                nc.vector.tensor_tensor(term[:], z[t][:].indirect(nxt_t[d][:]), gate2_t[:, d, :], MULT)
+                terms.append(term)
+            with_root = keep.tile([P, U], F32, name="with_root%d" % t, align_bytes=64)
+            if t < PACK - 1:
+                nc.vector.tensor_tensor(with_root[:], y[t][:].indirect(root_t[:]), terms[0][:], ADD)
+                sum_on_tensor([with_root, terms[1], terms[2]], U, 1.0, result[:, t, :])
+            else:
+                pair = keep.tile([P, U], F32, align_bytes=64)
+                nc.vector.tensor_add(pair[:], terms[0][:], terms[1][:])
+                nc.vector.tensor_tensor(with_root[:], y[t][:].indirect(root_t[:]), terms[2][:], ADD)
+                nc.vector.tensor_add(result[:, t, :], with_root[:], pair[:])
+            nc.sync.dma_start(out=out_rows[:, t, :], in_=result[:, t, :])
+
+        neighbours_1(0)
+        for t in range(1, PACK):
+            neighbours_1(t)
+            if t < PACK - 1:
+                restart_1(t - 1)
+        restart_1(PACK - 2)
+        step_2(0)
+        step_2(1)
+        restart_1(PACK - 1)
+        step_2(2)
+        step_2(3)
+
+        result_bf = keep.tile([P, U, PACK], BF16, align_bytes=64)
+        nc.vector.tensor_copy(
+            out=result_bf[:].rearrange("p (c i) t -> p c t i", i=4),
+            in_=result[:].rearrange("p t (c i) -> p c t i", i=4),
+        )
+        out_codes = keep.tile([P, U], U32, align_bytes=64)
+        out_sc = keep.tile([P, U], U8, align_bytes=64)
+        nc.vector.quantize_mx(
+            out=out_codes[:].bitcast(FP8X4),
+            scales=out_sc[:],
+            in_=result_bf[:].rearrange("p x t -> p (x t)"),
+        )
+        nc.sync.dma_start(
+            out=out_1[0].rearrange("p c r -> p (c r)").bitcast(I32),
+            in_=out_codes[:].bitcast(I32),
+        )
+        for q in range(4):
+            queue = nc.scalar if q % 2 == 0 else nc.sync
+            queue.dma_start(
+                out=out_2[0, 4 * q : 4 * q + 4, :].bitcast(I32),
+                in_=out_sc[32 * q : 32 * q + 4, :].bitcast(I32),
+            )

@@ -42,22 +42,23 @@ def tile_picked_zappnp_none_po_kernel(
             nc.sync.dma_start(tile[:], source)
             return tile
 
-        def load_scale_rows(tile, source):
-            nc.vector.memset(tile[:].bitcast(I32), 0)
+        def load_scale_rows(tile, source, queue):
             for q in range(4):
-                nc.gpsimd.dma_start(
+                queue.dma_start(
                     out=tile[32 * q : 32 * q + 4, :].bitcast(I32),
                     in_=source[0, 4 * q : 4 * q + 4, :].bitcast(I32),
                 )
 
         x_scale_table = keep.tile([P, T], U8, tag="x_bytes", align_bytes=64)
-        load_scale_rows(x_scale_table, x_scales)
-        w2_scale_rows = keep.tile([P, N], U8, align_bytes=64)
-        load_scale_rows(w2_scale_rows, w2_scales)
-
+        nc.gpsimd.memset(x_scale_table[:, : T // 2].bitcast(I32), 0)
+        nc.vector.memset(x_scale_table[:, T // 2 :].bitcast(I32), 0)
         w1_raw = keep.tile([P, PACK, H], F32, align_bytes=64)
         nc.sync.dma_start(out=w1_raw[:], in_=w1.rearrange("(p j) c -> p j c", j=PACK))
         offs_t = load_list("offs_t", offs)
+        load_scale_rows(x_scale_table, x_scales, nc.sync)
+        w2_scale_rows = keep.tile([P, N], U8, align_bytes=64)
+        nc.vector.memset(w2_scale_rows[:].bitcast(I32), 0)
+
         x_word_table = keep.tile([P, T], U32, align_bytes=64)
         nc.sync.dma_start(
             out=x_word_table[:].bitcast(I32),
@@ -65,6 +66,7 @@ def tile_picked_zappnp_none_po_kernel(
         )
         w2_raw = keep.tile([P, N], I32, align_bytes=64)
         nc.sync.dma_start(out=w2_raw[:], in_=w2_words[0].rearrange("p c r -> p (c r)").bitcast(I32))
+        load_scale_rows(w2_scale_rows, w2_scales, nc.sync)
         gate_t = keep.tile([P, D, V], F32, align_bytes=64)
         nc.sync.dma_start(out=gate_t[:], in_=gate.rearrange("d p v -> p d v"))
         pos_t = [load_list("pos%d_t" % d, src) for d, src in enumerate((pos1, pos2, pos3))]
@@ -97,17 +99,28 @@ def tile_picked_zappnp_none_po_kernel(
 
         x_sc = keep.tile([P, S], U8, align_bytes=64)
         nc.vector.tensor_copy(x_sc[:], x_scale_table[:].indirect(offs_t[:]))
+        for t in range(PACK):
+            warm = psum.tile([P, HALF], F32, name="warm", tag="b")
+            nc.tensor.matmul_mx(
+                out=warm[:],
+                lhsT=w1_codes[:, t * P : (t + 1) * P].bitcast(FP8X4),
+                lhsT_scale=w1_sc[:, t * P : (t + 1) * P],
+                rhs=w1_codes[:].bitcast(FP8X4),
+                rhs_scale=x_sc[:, :HALF],
+                start=True,
+                stop=True,
+            )
         x_codes = keep.tile([P, S], U32, tag="x_bytes", align_bytes=64)
-        w2_sc = keep.tile([P, PACK, P], U8, align_bytes=64)
-        nc.vector.tensor_copy(
-            out=w2_sc[:].rearrange("p t m -> p m t"),
-            in_=w2_scale_rows[:].rearrange("p (m t) -> p m t", t=PACK),
-        )
         for u in range(2):
             nc.vector.tensor_copy(
                 x_codes[:, u * HALF : (u + 1) * HALF],
                 x_word_table[:].indirect(offs_t[:, u * HALF // 16 : (u + 1) * HALF // 16]),
             )
+        w2_sc = keep.tile([P, PACK, P], U8, align_bytes=64)
+        nc.vector.tensor_copy(
+            out=w2_sc[:].rearrange("p t m -> p m t"),
+            in_=w2_scale_rows[:].rearrange("p (m t) -> p m t", t=PACK),
+        )
         w2_codes = keep.tile([P, PACK, P], I32, align_bytes=64)
         nc.vector.tensor_copy(
             out=w2_codes[:].rearrange("p t m -> p m t"),

@@ -21,9 +21,9 @@ P = 128
 PACK = 4
 HALF = S // 2
 CHUNK = 128
-PIECE = 256
-VECTOR_CHUNKS = (5, 7)
-VECTOR_PIECES = (3,)
+PIECES = ((0, 512), (512, 768), (768, 1024))
+VECTOR_CHUNKS = (1, 4, 6)
+FIRST_WORDS = 1536
 
 
 def tile_picked_zappnp_none_po_kernel(
@@ -52,19 +52,24 @@ def tile_picked_zappnp_none_po_kernel(
         x_scale_table = keep.tile([P, T], U8, tag="x_bytes", align_bytes=64)
         nc.gpsimd.memset(x_scale_table[:, : T // 2].bitcast(I32), 0)
         nc.vector.memset(x_scale_table[:, T // 2 :].bitcast(I32), 0)
-        w1_raw = keep.tile([P, PACK, H], F32, align_bytes=64)
-        nc.sync.dma_start(out=w1_raw[:], in_=w1.rearrange("(p j) c -> p j c", j=PACK))
+        x_word_table = keep.tile([P, T], U32, tag="x_table", align_bytes=64)
+        x_word_rows = x_words[0].rearrange("p c r -> p (c r)").bitcast(I32)
+        nc.sync.dma_start(out=x_word_table[:, :FIRST_WORDS].bitcast(I32), in_=x_word_rows[:, :FIRST_WORDS])
         offs_t = load_list("offs_t", offs)
         load_scale_rows(x_scale_table, x_scales, nc.sync)
         w2_scale_rows = keep.tile([P, N], U8, align_bytes=64)
         nc.vector.memset(w2_scale_rows[:].bitcast(I32), 0)
 
-        x_word_table = keep.tile([P, T], U32, align_bytes=64)
-        nc.sync.dma_start(
-            out=x_word_table[:].bitcast(I32),
-            in_=x_words[0].rearrange("p c r -> p (c r)").bitcast(I32),
-        )
-        w2_raw = keep.tile([P, N], I32, align_bytes=64)
+        nc.sync.dma_start(out=x_word_table[:, FIRST_WORDS:].bitcast(I32), in_=x_word_rows[:, FIRST_WORDS:])
+        w1_raw = []
+        for half in range(2):
+            part = keep.tile([P, PACK, H // 2], F32, name="w1_raw%d" % half, align_bytes=64)
+            nc.sync.dma_start(
+                out=part[:],
+                in_=w1.rearrange("(p j) c -> p j c", j=PACK)[:, :, half * H // 2 : (half + 1) * H // 2],
+            )
+            w1_raw.append(part)
+        w2_raw = keep.tile([P, N], I32, tag="w2_raw", align_bytes=64)
         nc.sync.dma_start(out=w2_raw[:], in_=w2_words[0].rearrange("p c r -> p (c r)").bitcast(I32))
         load_scale_rows(w2_scale_rows, w2_scales, nc.sync)
         gate_t = keep.tile([P, D, V], F32, align_bytes=64)
@@ -79,64 +84,67 @@ def tile_picked_zappnp_none_po_kernel(
         identity = keep.tile([P, P], F32, align_bytes=64)
         make_identity(nc, identity[:])
 
-        w1_codes = keep.tile([P, H], U32, align_bytes=64)
-        w1_sc = keep.tile([P, H], U8, align_bytes=64)
-        w1_view = w1_raw[:].rearrange("p j (m t) -> p m t j", t=PACK)
-        for u in range(2):
-            w1_bf = keep.tile([P, 2, P, PACK], BF16, name="w1_bf%d" % u, align_bytes=64)
-            dst = w1_bf[:].rearrange("p t m j -> p m t j")
-            src = w1_view[:, :, 2 * u : 2 * u + 2, :]
-            if u == 0:
-                nc.vector.tensor_copy(out=dst, in_=src)
-            else:
-                nc.scalar.activation(out=dst, in_=src, func=COPY)
-            cols = slice(2 * P * u, 2 * P * (u + 1))
-            nc.vector.quantize_mx(
-                out=w1_codes[:, cols].bitcast(FP8X4),
-                scales=w1_sc[:, cols],
-                in_=w1_bf[:].rearrange("p t m j -> p (t m j)"),
-            )
-
         x_sc = keep.tile([P, S], U8, align_bytes=64)
         nc.vector.tensor_copy(x_sc[:], x_scale_table[:].indirect(offs_t[:]))
-        for t in range(PACK):
-            warm = psum.tile([P, HALF], F32, name="warm", tag="b")
-            nc.tensor.matmul_mx(
-                out=warm[:],
-                lhsT=w1_codes[:, t * P : (t + 1) * P].bitcast(FP8X4),
-                lhsT_scale=w1_sc[:, t * P : (t + 1) * P],
-                rhs=w1_codes[:].bitcast(FP8X4),
-                rhs_scale=x_sc[:, :HALF],
-                start=True,
-                stop=True,
-            )
         x_codes = keep.tile([P, S], U32, tag="x_bytes", align_bytes=64)
         for u in range(2):
             nc.vector.tensor_copy(
                 x_codes[:, u * HALF : (u + 1) * HALF],
                 x_word_table[:].indirect(offs_t[:, u * HALF // 16 : (u + 1) * HALF // 16]),
             )
-        w2_sc = keep.tile([P, PACK, P], U8, align_bytes=64)
-        nc.vector.tensor_copy(
-            out=w2_sc[:].rearrange("p t m -> p m t"),
-            in_=w2_scale_rows[:].rearrange("p (m t) -> p m t", t=PACK),
-        )
-        w2_codes = keep.tile([P, PACK, P], I32, align_bytes=64)
+        for t in range(PACK):
+            warm = psum.tile([P, HALF], F32, name="warm", tag="b")
+            nc.tensor.matmul_mx(
+                out=warm[:],
+                lhsT=x_codes[:, t * P : (t + 1) * P].bitcast(FP8X4),
+                lhsT_scale=x_sc[:, t * P : (t + 1) * P],
+                rhs=x_codes[:, :HALF].bitcast(FP8X4),
+                rhs_scale=x_sc[:, :HALF],
+                start=True,
+                stop=True,
+            )
+
+        w1_codes = keep.tile([P, H], U32, align_bytes=64)
+        w1_sc = keep.tile([P, H], U8, align_bytes=64)
+        w1_bf = [
+            keep.tile([P, 2, P, PACK], BF16, name="w1_bf", tag="w1_bf%d" % u, align_bytes=64) for u in range(2)
+        ]
+        for half in range(2):
+            for u in range(2):
+                dst = w1_bf[u][:, :, half * P // 2 : (half + 1) * P // 2, :].rearrange("p t m j -> p m t j")
+                src = w1_raw[half][:].rearrange("p j (m t) -> p m t j", t=PACK)[:, :, 2 * u : 2 * u + 2, :]
+                if (half, u) == (1, 0):
+                    nc.vector.tensor_copy(out=dst, in_=src)
+                else:
+                    nc.scalar.activation(out=dst, in_=src, func=COPY)
+        for u in range(2):
+            cols = slice(2 * P * u, 2 * P * (u + 1))
+            nc.vector.quantize_mx(
+                out=w1_codes[:, cols].bitcast(FP8X4),
+                scales=w1_sc[:, cols],
+                in_=w1_bf[u][:].rearrange("p t m j -> p (t m j)"),
+            )
+
+        w2_codes = keep.tile([P, PACK, P], I32, tag="w1_bf1", align_bytes=64)
         nc.vector.tensor_copy(
             out=w2_codes[:].rearrange("p t m -> p m t"),
             in_=w2_raw[:].rearrange("p (m t) -> p m t", t=PACK),
         )
+        w2_scale_view = w2_scale_rows[:].rearrange("p (m t) -> p m t", t=PACK)
+        w2_sc_first = keep.tile([P, P], U8, tag="w2_raw", align_bytes=64)
+        nc.vector.tensor_copy(out=w2_sc_first[:], in_=w2_scale_view[:, :, 0])
+        w2_sc = [w2_sc_first[:]]
 
         h_codes = keep.tile([P, S], U32, align_bytes=64)
         h_sc = keep.tile([P, S], U8, align_bytes=64)
         y = [keep.tile([P, S], F32, name="y%d" % t, align_bytes=64) for t in range(PACK)]
 
         def second_layer(t, cols, on_vector):
-            bank = psum.tile([P, cols.stop - cols.start], F32, name="y_bank", tag="b")
+            bank = psum.tile([P, cols.stop - cols.start], F32, name="y_bank", tag="a" if t == 0 else "b")
             nc.tensor.matmul_mx(
                 out=bank[:],
                 lhsT=w2_codes[:, t, :].bitcast(FP8X4),
-                lhsT_scale=w2_sc[:, t, :],
+                lhsT_scale=w2_sc[t],
                 rhs=h_codes[:, cols].bitcast(FP8X4),
                 rhs_scale=h_sc[:, cols],
                 start=True,
@@ -147,12 +155,14 @@ def tile_picked_zappnp_none_po_kernel(
             else:
                 nc.scalar.activation(out=y[t][:, cols], in_=bank[:], func=COPY, scale=0.2)
 
-        for piece in range(S // PIECE):
-            h_bf = keep.tile([P, PIECE, PACK], BF16, name="h_bf", tag="h_bf%d" % piece, align_bytes=64)
-            for c in range(PIECE // CHUNK):
-                chunk = piece * (PIECE // CHUNK) + c
-                cols = slice(chunk * CHUNK, (chunk + 1) * CHUNK)
-                bank = psum.tile([P, PACK, CHUNK], F32, name="h_bank", tag="a")
+        h_bf = [
+            keep.tile([P, b - a, PACK], BF16, name="h_bf", tag="h_bf%d" % i, align_bytes=64)
+            for i, (a, b) in enumerate(PIECES)
+        ]
+        for i, (a, b) in enumerate(PIECES):
+            for first in range(a, b, CHUNK):
+                cols = slice(first, first + CHUNK)
+                bank = psum.tile([P, PACK, CHUNK], F32, name="h_bank", tag="a" if first < HALF else "b")
                 for t in range(PACK):
                     nc.tensor.matmul_mx(
                         out=bank[:, t, :],
@@ -163,100 +173,124 @@ def tile_picked_zappnp_none_po_kernel(
                         start=True,
                         stop=True,
                     )
-                dst = h_bf[:, c * CHUNK : (c + 1) * CHUNK, :]
+                dst = h_bf[i][:, first - a : first - a + CHUNK, :]
                 src = bank[:].rearrange("p t n -> p n t")
-                if chunk in VECTOR_CHUNKS:
+                if first // CHUNK in VECTOR_CHUNKS:
                     nc.vector.tensor_copy(out=dst, in_=src)
                 else:
                     nc.scalar.copy(out=dst, in_=src)
-            cols = slice(piece * PIECE, (piece + 1) * PIECE)
+        for i, (a, b) in enumerate(PIECES):
+            cols = slice(a, b)
             nc.vector.quantize_mx(
                 out=h_codes[:, cols].bitcast(FP8X4),
                 scales=h_sc[:, cols],
-                in_=h_bf[:].rearrange("p n t -> p (n t)"),
+                in_=h_bf[i][:].rearrange("p n t -> p (n t)"),
             )
-            second_layer(0, cols, piece in VECTOR_PIECES)
+        for i, (a, b) in enumerate(PIECES):
+            second_layer(0, slice(a, b), i == 1)
+        w2_sc_rest = keep.tile([P, PACK - 1, P], U8, tag="h_bf%d" % (len(PIECES) - 1), align_bytes=64)
+        nc.vector.tensor_copy(out=w2_sc_rest[:].rearrange("p t m -> p m t"), in_=w2_scale_view[:, :, 1:])
+        w2_sc.extend(w2_sc_rest[:, t, :] for t in range(PACK - 1))
         for t in range(1, PACK):
             for u in range(2):
                 second_layer(t, slice(u * HALF, (u + 1) * HALF), False)
 
-        gate2_t = keep.tile([P, D, U], F32, name="gate2_t", tag="h_bf%d" % (S // PIECE - 1), align_bytes=64)
-        nc.scalar.activation(out=gate2_t[:], in_=gate2_raw[:], func=COPY, scale=0.8)
 
-        def sum_on_tensor(terms, width, scale, dst):
-            turned = psum.tile([P, width], F32, name="turned", tag="a")
-            for b in range(width // P):
-                cols = slice(b * P, (b + 1) * P)
-                for i, term in enumerate(terms):
+        def sum_on_tensor(terms, width, scale, dst, tag):
+            blocks = [slice(b * P, (b + 1) * P) for b in range(width // P)]
+            banks = [psum.tile([P, P], F32, name="turned", tag="a") for cols in blocks]
+            for i, term in enumerate(terms):
+                for bank, cols in zip(banks, blocks):
                     nc.tensor.matmul(
-                        turned[:, cols], term[:, cols], identity[:],
+                        bank[:], term[:, cols], identity[:],
                         start=(i == 0), stop=(i == len(terms) - 1), is_transpose=True,
                     )
-            turned_sb = ring.tile([P, width], F32, name="turned_sb", align_bytes=64)
-            nc.scalar.activation(out=turned_sb[:], in_=turned[:], func=COPY, scale=scale)
+            pool = ring if tag == "turned_sb" else keep
+            turned_sb = pool.tile([P, width], F32, name="turned_sb", tag=tag, align_bytes=64)
             back = psum.tile([P, width], F32, name="back", tag="b")
-            for b in range(width // P):
-                cols = slice(b * P, (b + 1) * P)
+            for bank, cols in zip(banks, blocks):
+                nc.scalar.activation(out=turned_sb[:, cols], in_=bank[:], func=COPY, scale=scale)
+            for cols in blocks:
                 nc.tensor.transpose(back[:, cols], turned_sb[:, cols], identity[:])
             nc.scalar.copy(out=dst, in_=back[:])
 
-        z = [keep.tile([P, V], F32, name="z%d" % t, align_bytes=64) for t in range(PACK)]
-        mixed = [keep.tile([P, V], F32, name="mixed%d" % t, align_bytes=64) for t in range(PACK)]
-        result = keep.tile([P, PACK, U], F32, align_bytes=64)
+        z = [keep.tile([P, V], F32, name="z", tag="z%d" % t, align_bytes=64) for t in range(PACK)]
+        mixed = [keep.tile([P, V], F32, name="mixed", tag="mixed%d" % t, align_bytes=64) for t in range(PACK)]
         out_rows = out_0.rearrange("(p t) x -> p t x", t=PACK)
 
         def neighbours_1(t):
             terms = []
             for d in range(D):
-                term = keep.tile([P, V], F32, name="near%d_%d" % (t, d), align_bytes=64)
+                term = keep.tile([P, V], F32, name="near", tag="near%d_%d" % (t, d), align_bytes=64)
                 nc.vector.tensor_tensor(term[:], y[t][:].indirect(pos_t[d][:]), gate_t[:, d, :], MULT)
                 terms.append(term)
-            sum_on_tensor(terms, V, 4.0, mixed[t][:])
+            sum_on_tensor(terms, V, 4.0, mixed[t][:], "turned_sb")
 
         def restart_1(t):
             nc.vector.tensor_tensor(z[t][:], y[t][:].indirect(cen_t[:]), mixed[t][:], ADD)
 
-        def step_2(t):
-            terms = []
+        mixed2 = [keep.tile([P, U], F32, name="mixed2_%d" % t, align_bytes=64) for t in range(PACK)]
+        halves = [slice(0, U // 2), slice(U // 2, U)]
+
+        def neighbours_2(t, cols, tag):
             for d in range(D):
-                term = keep.tile([P, U], F32, name="far%d_%d" % (t, d), align_bytes=64)
-                nc.vector.tensor_tensor(term[:], z[t][:].indirect(nxt_t[d][:]), gate2_t[:, d, :], MULT)
-                terms.append(term)
-            with_root = keep.tile([P, U], F32, name="with_root%d" % t, align_bytes=64)
-            if t < PACK - 1:
-                nc.vector.tensor_tensor(with_root[:], y[t][:].indirect(root_t[:]), terms[0][:], ADD)
-                sum_on_tensor([with_root, terms[1], terms[2]], U, 1.0, result[:, t, :])
-            else:
-                pair = keep.tile([P, U], F32, align_bytes=64)
-                nc.vector.tensor_add(pair[:], terms[0][:], terms[1][:])
-                nc.vector.tensor_tensor(with_root[:], y[t][:].indirect(root_t[:]), terms[2][:], ADD)
-                nc.vector.tensor_add(result[:, t, :], with_root[:], pair[:])
-            nc.sync.dma_start(out=out_rows[:, t, :], in_=result[:, t, :])
+                nc.vector.tensor_tensor(
+                    far[:, t, d, cols],
+                    z[t][:].indirect(nxt_t[d][:, cols.start // 16 : cols.stop // 16]),
+                    gate2_t[:, d, cols],
+                    MULT,
+                )
+            terms = [far[:, t, d, cols] for d in range(D)]
+            sum_on_tensor(terms, cols.stop - cols.start, 1.0, mixed2[t][:, cols], tag)
 
-        neighbours_1(0)
-        for t in range(1, PACK):
+        def restart_2(t, cols):
+            nc.vector.tensor_tensor(
+                result[:, t, cols],
+                y[t][:].indirect(root_t[:, cols.start // 16 : cols.stop // 16]),
+                mixed2[t][:, cols],
+                ADD,
+            )
+
+        last = PACK - 1
+        for t in range(PACK):
             neighbours_1(t)
-            if t < PACK - 1:
-                restart_1(t - 1)
-        restart_1(PACK - 2)
-        step_2(0)
-        step_2(1)
-        restart_1(PACK - 1)
-        step_2(2)
-        step_2(3)
+        gate2_t = keep.tile([P, D, U], F32, name="gate2_t", tag="near0_0", align_bytes=64)
+        nc.scalar.activation(out=gate2_t[:], in_=gate2_raw[:], func=COPY, scale=0.8)
+        for t in range(PACK):
+            restart_1(t)
+        far = keep.tile([P, PACK, D, U], F32, name="far", tag="mixed%d" % last, align_bytes=64)
+        for t in range(last):
+            neighbours_2(t, slice(0, U), "turned_sb")
+        neighbours_2(last, halves[0], "turned_sb")
+        neighbours_2(last, halves[1], "last_turned")
 
-        result_bf = keep.tile([P, U, PACK], BF16, align_bytes=64)
-        nc.vector.tensor_copy(
-            out=result_bf[:].rearrange("p (c i) t -> p c t i", i=4),
-            in_=result[:].rearrange("p t (c i) -> p c t i", i=4),
-        )
+        result = keep.tile([P, PACK, U], F32, name="result", tag="near0_0", align_bytes=64)
+        for t in range(last):
+            restart_2(t, slice(0, U))
+            nc.sync.dma_start(out=out_rows[:, t, :], in_=result[:, t, :])
+        for cols in halves:
+            restart_2(last, cols)
+        nc.sync.dma_start(out=out_rows[:, last, :], in_=result[:, last, :])
+
         out_codes = keep.tile([P, U], U32, align_bytes=64)
         out_sc = keep.tile([P, U], U8, align_bytes=64)
-        nc.vector.quantize_mx(
-            out=out_codes[:].bitcast(FP8X4),
-            scales=out_sc[:],
-            in_=result_bf[:].rearrange("p x t -> p (x t)"),
-        )
+        result_bf = [
+            keep.tile([P, U // 2, PACK], BF16, name="result_bf", tag=tag, align_bytes=64)
+            for tag in ("last_turned", "result_bf")
+        ]
+        for u, cols in enumerate(halves):
+            dst = result_bf[u][:].rearrange("p (c i) t -> p c t i", i=4)
+            src = result[:, :, cols].rearrange("p t (c i) -> p c t i", i=4)
+            if u == 0:
+                nc.scalar.copy(out=dst, in_=src)
+            else:
+                nc.vector.tensor_copy(out=dst, in_=src)
+        for u, cols in enumerate(halves):
+            nc.vector.quantize_mx(
+                out=out_codes[:, cols].bitcast(FP8X4),
+                scales=out_sc[:, cols],
+                in_=result_bf[u][:].rearrange("p x t -> p (x t)"),
+            )
         nc.sync.dma_start(
             out=out_1[0].rearrange("p c r -> p (c r)").bitcast(I32),
             in_=out_codes[:].bitcast(I32),

@@ -43,22 +43,21 @@ def tile_picked_zappnp_none_po_kernel(
             return tile
 
         def load_scale_rows(tile, source, queue):
-            for q in range(4):
+            for r in range(4):
                 queue.dma_start(
-                    out=tile[32 * q : 32 * q + 4, :].bitcast(I32),
-                    in_=source[0, 4 * q : 4 * q + 4, :].bitcast(I32),
+                    out=tile[r:P:32, :].bitcast(I32),
+                    in_=source[0, r:16:4, :].bitcast(I32),
                 )
 
         x_scale_table = keep.tile([P, T], U8, tag="x_bytes", align_bytes=64)
-        nc.gpsimd.memset(x_scale_table[:, : T // 2].bitcast(I32), 0)
-        nc.vector.memset(x_scale_table[:, T // 2 :].bitcast(I32), 0)
+        nc.gpsimd.memset(x_scale_table[:].bitcast(I32), 0)
         x_word_table = keep.tile([P, T], U32, tag="x_table", align_bytes=64)
         x_word_rows = x_words[0].rearrange("p c r -> p (c r)").bitcast(I32)
         nc.sync.dma_start(out=x_word_table[:, :FIRST_WORDS].bitcast(I32), in_=x_word_rows[:, :FIRST_WORDS])
         offs_t = load_list("offs_t", offs)
         load_scale_rows(x_scale_table, x_scales, nc.sync)
         w2_scale_rows = keep.tile([P, N], U8, align_bytes=64)
-        nc.vector.memset(w2_scale_rows[:].bitcast(I32), 0)
+        nc.gpsimd.memset(w2_scale_rows[:].bitcast(I32), 0)
 
         nc.sync.dma_start(out=x_word_table[:, FIRST_WORDS:].bitcast(I32), in_=x_word_rows[:, FIRST_WORDS:])
         w1_raw = []

@@ -83,6 +83,9 @@ def tile_picked_zappnp_none_po_kernel(
         identity = keep.tile([P, P], F32, align_bytes=64)
         make_identity(nc, identity[:])
 
+        quarter = keep.tile([P, V], F32, align_bytes=64)
+        nc.gpsimd.memset(quarter[:], 0.25)
+
         x_sc = keep.tile([P, S], U8, align_bytes=64)
         nc.vector.tensor_copy(x_sc[:], x_scale_table[:].indirect(offs_t[:]))
         x_codes = keep.tile([P, S], U32, tag="x_bytes", align_bytes=64)
@@ -214,7 +217,6 @@ def tile_picked_zappnp_none_po_kernel(
             nc.scalar.copy(out=dst, in_=back[:])
 
         z = [keep.tile([P, V], F32, name="z", tag="z%d" % t, align_bytes=64) for t in range(PACK)]
-        mixed = [keep.tile([P, V], F32, name="mixed", tag="mixed%d" % t, align_bytes=64) for t in range(PACK)]
         out_rows = out_0.rearrange("(p t) x -> p t x", t=PACK)
 
         def neighbours_1(t):
@@ -223,10 +225,9 @@ def tile_picked_zappnp_none_po_kernel(
                 term = keep.tile([P, V], F32, name="near", tag="near%d_%d" % (t, d), align_bytes=64)
                 nc.vector.tensor_tensor(term[:], y[t][:].indirect(pos_t[d][:]), gate_t[:, d, :], MULT)
                 terms.append(term)
-            sum_on_tensor(terms, V, 4.0, mixed[t][:], "turned_sb")
-
-        def restart_1(t):
-            nc.vector.tensor_tensor(z[t][:], y[t][:].indirect(cen_t[:]), mixed[t][:], ADD)
+            own = keep.tile([P, V], F32, name="own", tag="own%d" % t, align_bytes=64)
+            nc.vector.tensor_tensor(own[:], y[t][:].indirect(cen_t[:]), quarter[:], MULT)
+            sum_on_tensor(terms + [own], V, 4.0, z[t][:], "turned_sb")
 
         mixed2 = [keep.tile([P, U], F32, name="mixed2_%d" % t, align_bytes=64) for t in range(PACK)]
         halves = [slice(0, U // 2), slice(U // 2, U)]
@@ -255,9 +256,7 @@ def tile_picked_zappnp_none_po_kernel(
             neighbours_1(t)
         gate2_t = keep.tile([P, D, U], F32, name="gate2_t", tag="near0_0", align_bytes=64)
         nc.scalar.activation(out=gate2_t[:], in_=gate2_raw[:], func=COPY, scale=0.8)
-        for t in range(PACK):
-            restart_1(t)
-        far = keep.tile([P, PACK, D, U], F32, name="far", tag="mixed%d" % last, align_bytes=64)
+        far = keep.tile([P, PACK, D, U], F32, name="far", align_bytes=64)
         for t in range(last):
             neighbours_2(t, slice(0, U), "turned_sb")
         neighbours_2(last, halves[0], "turned_sb")

@@ -21,8 +21,11 @@ P = 128
 PACK = 4
 HALF = S // 2
 CHUNK = 128
-PIECES = ((0, 512), (512, 768), (768, 1024))
-VECTOR_CHUNKS = (1, 4, 6)
+PIECES = ((0, 512), (512, 768), (768, 896), (896, 1024))
+PIECE_ORDER = (0, 1, 2, 3)
+VECTOR_CHUNKS = (3, 6)
+VECTOR_PIECES = (1,)
+WARM = 3
 FIRST_WORDS = 1536
 
 
@@ -49,6 +52,14 @@ def tile_picked_zappnp_none_po_kernel(
                     in_=source[0, r:16:4, :].bitcast(I32),
                 )
 
+        def load_w1_half(half):
+            part = keep.tile([P, PACK, H // 2], F32, name="w1_raw%d" % half, align_bytes=64)
+            nc.sync.dma_start(
+                out=part[:],
+                in_=w1.rearrange("(p j) c -> p j c", j=PACK)[:, :, half * H // 2 : (half + 1) * H // 2],
+            )
+            return part
+
         x_scale_table = keep.tile([P, T], U8, tag="x_bytes", align_bytes=64)
         nc.gpsimd.memset(x_scale_table[:].bitcast(I32), 0)
         x_word_table = keep.tile([P, T], U32, tag="x_table", align_bytes=64)
@@ -56,25 +67,17 @@ def tile_picked_zappnp_none_po_kernel(
         nc.sync.dma_start(out=x_word_table[:, :FIRST_WORDS].bitcast(I32), in_=x_word_rows[:, :FIRST_WORDS])
         offs_t = load_list("offs_t", offs)
         load_scale_rows(x_scale_table, x_scales, nc.sync)
+        nc.sync.dma_start(out=x_word_table[:, FIRST_WORDS:].bitcast(I32), in_=x_word_rows[:, FIRST_WORDS:])
+        w1_raw = [load_w1_half(half) for half in range(2)]
         w2_scale_rows = keep.tile([P, N], U8, align_bytes=64)
         nc.gpsimd.memset(w2_scale_rows[:].bitcast(I32), 0)
-
-        nc.sync.dma_start(out=x_word_table[:, FIRST_WORDS:].bitcast(I32), in_=x_word_rows[:, FIRST_WORDS:])
-        w1_raw = []
-        for half in range(2):
-            part = keep.tile([P, PACK, H // 2], F32, name="w1_raw%d" % half, align_bytes=64)
-            nc.sync.dma_start(
-                out=part[:],
-                in_=w1.rearrange("(p j) c -> p j c", j=PACK)[:, :, half * H // 2 : (half + 1) * H // 2],
-            )
-            w1_raw.append(part)
         w2_raw = keep.tile([P, N], I32, tag="w2_raw", align_bytes=64)
         nc.sync.dma_start(out=w2_raw[:], in_=w2_words[0].rearrange("p c r -> p (c r)").bitcast(I32))
         load_scale_rows(w2_scale_rows, w2_scales, nc.sync)
-        gate_t = keep.tile([P, D, V], F32, align_bytes=64)
-        nc.sync.dma_start(out=gate_t[:], in_=gate.rearrange("d p v -> p d v"))
         pos_t = [load_list("pos%d_t" % d, src) for d, src in enumerate((pos1, pos2, pos3))]
         cen_t = load_list("cen_t", cen)
+        gate_t = keep.tile([P, D, V], F32, align_bytes=64)
+        nc.sync.dma_start(out=gate_t[:], in_=gate.rearrange("d p v -> p d v"))
         nxt_t = [load_list("nxt%d_t" % d, src) for d, src in enumerate((nxt1, nxt2, nxt3))]
         root_t = load_list("root_t", root)
         gate2_raw = keep.tile([P, D, U], F32, align_bytes=64)
@@ -86,66 +89,101 @@ def tile_picked_zappnp_none_po_kernel(
         quarter = keep.tile([P, V], F32, align_bytes=64)
         nc.gpsimd.memset(quarter[:], 0.25)
 
+        w1_codes = keep.tile([P, H], U32, align_bytes=64)
+        w1_sc = keep.tile([P, H], U8, align_bytes=64)
+
+        def round_w1(half, u, on_vector):
+            dealt = keep.tile(
+                [P, 2, P // 2, PACK], BF16, name="w1_bf", tag="w1_bf%d_%d" % (half, u), align_bytes=64
+            )
+            dst = dealt[:].rearrange("p t m j -> p m t j")
+            src = w1_raw[half][:].rearrange("p j (m t) -> p m t j", t=PACK)[:, :, 2 * u : 2 * u + 2, :]
+            if on_vector:
+                nc.vector.tensor_copy(out=dst, in_=src)
+            else:
+                nc.scalar.activation(out=dst, in_=src, func=COPY)
+            return dealt
+
+        def quantise_w1(half, u, dealt):
+            for i in range(2):
+                first = (2 * u + i) * P + half * P // 2
+                cols = slice(first, first + P // 2)
+                nc.vector.quantize_mx(
+                    out=w1_codes[:, cols].bitcast(FP8X4),
+                    scales=w1_sc[:, cols],
+                    in_=dealt[:, i, :, :].rearrange("p m j -> p (m j)"),
+                )
+
+        def gather_words(u, tag):
+            codes = keep.tile([P, HALF], U32, name="x_codes", tag=tag, align_bytes=64)
+            nc.vector.tensor_copy(
+                codes[:], x_word_table[:].indirect(offs_t[:, u * HALF // 16 : (u + 1) * HALF // 16])
+            )
+            return codes
+
         x_sc = keep.tile([P, S], U8, align_bytes=64)
         nc.vector.tensor_copy(x_sc[:], x_scale_table[:].indirect(offs_t[:]))
-        x_codes = keep.tile([P, S], U32, tag="x_bytes", align_bytes=64)
-        for u in range(2):
-            nc.vector.tensor_copy(
-                x_codes[:, u * HALF : (u + 1) * HALF],
-                x_word_table[:].indirect(offs_t[:, u * HALF // 16 : (u + 1) * HALF // 16]),
-            )
-        for t in range(PACK):
+        x_codes = [gather_words(0, "x_bytes")]
+        for t in range(WARM):
             warm = psum.tile([P, HALF], F32, name="warm", tag="b")
             nc.tensor.matmul_mx(
                 out=warm[:],
-                lhsT=x_codes[:, t * P : (t + 1) * P].bitcast(FP8X4),
+                lhsT=x_codes[0][:, t * P : (t + 1) * P].bitcast(FP8X4),
                 lhsT_scale=x_sc[:, t * P : (t + 1) * P],
-                rhs=x_codes[:, :HALF].bitcast(FP8X4),
+                rhs=x_codes[0][:].bitcast(FP8X4),
                 rhs_scale=x_sc[:, :HALF],
                 start=True,
                 stop=True,
             )
-
-        w1_codes = keep.tile([P, H], U32, align_bytes=64)
-        w1_sc = keep.tile([P, H], U8, align_bytes=64)
-        w1_bf = [
-            keep.tile([P, 2, P, PACK], BF16, name="w1_bf", tag="w1_bf%d" % u, align_bytes=64) for u in range(2)
-        ]
         for half in range(2):
+            late = [round_w1(half, u, u == 0) for u in range(2)]
             for u in range(2):
-                dst = w1_bf[u][:, :, half * P // 2 : (half + 1) * P // 2, :].rearrange("p t m j -> p m t j")
-                src = w1_raw[half][:].rearrange("p j (m t) -> p m t j", t=PACK)[:, :, 2 * u : 2 * u + 2, :]
-                if (half, u) == (1, 0):
-                    nc.vector.tensor_copy(out=dst, in_=src)
-                else:
-                    nc.scalar.activation(out=dst, in_=src, func=COPY)
-        for u in range(2):
-            cols = slice(2 * P * u, 2 * P * (u + 1))
-            nc.vector.quantize_mx(
-                out=w1_codes[:, cols].bitcast(FP8X4),
-                scales=w1_sc[:, cols],
-                in_=w1_bf[u][:].rearrange("p t m j -> p (t m j)"),
-            )
-
-        w2_codes = keep.tile([P, PACK, P], I32, tag="w1_bf1", align_bytes=64)
-        nc.vector.tensor_copy(
-            out=w2_codes[:].rearrange("p t m -> p m t"),
-            in_=w2_raw[:].rearrange("p (m t) -> p m t", t=PACK),
-        )
-        w2_scale_view = w2_scale_rows[:].rearrange("p (m t) -> p m t", t=PACK)
-        w2_sc_first = keep.tile([P, P], U8, tag="w2_raw", align_bytes=64)
-        nc.vector.tensor_copy(out=w2_sc_first[:], in_=w2_scale_view[:, :, 0])
-        w2_sc = [w2_sc_first[:]]
+                quantise_w1(half, u, late[u])
+        x_codes.append(gather_words(1, "w1_bf1_1"))
 
         h_codes = keep.tile([P, S], U32, align_bytes=64)
         h_sc = keep.tile([P, S], U8, align_bytes=64)
         y = [keep.tile([P, S], F32, name="y%d" % t, align_bytes=64) for t in range(PACK)]
+        h_bf = [
+            keep.tile([P, b - a, PACK], BF16, name="h_bf", tag="h_bf%d" % i, align_bytes=64)
+            for i, (a, b) in enumerate(PIECES)
+        ]
+
+        def first_layer(chunk):
+            first = chunk * CHUNK
+            piece = max(i for i, (a, b) in enumerate(PIECES) if a <= first)
+            within = first - PIECES[piece][0]
+            bank = psum.tile([P, PACK, CHUNK], F32, name="h_bank", tag="a" if first < HALF else "b")
+            for t in reversed(range(PACK)):
+                nc.tensor.matmul_mx(
+                    out=bank[:, t, :],
+                    lhsT=w1_codes[:, t * P : (t + 1) * P].bitcast(FP8X4),
+                    lhsT_scale=w1_sc[:, t * P : (t + 1) * P],
+                    rhs=x_codes[first // HALF][:, first % HALF : first % HALF + CHUNK].bitcast(FP8X4),
+                    rhs_scale=x_sc[:, first : first + CHUNK],
+                    start=True,
+                    stop=True,
+                )
+            dst = h_bf[piece][:, within : within + CHUNK, :]
+            src = bank[:].rearrange("p t n -> p n t")
+            if chunk in VECTOR_CHUNKS:
+                nc.vector.tensor_copy(out=dst, in_=src)
+            else:
+                nc.scalar.copy(out=dst, in_=src)
+
+        def quantise_hidden(piece):
+            cols = slice(*PIECES[piece])
+            nc.vector.quantize_mx(
+                out=h_codes[:, cols].bitcast(FP8X4),
+                scales=h_sc[:, cols],
+                in_=h_bf[piece][:].rearrange("p n t -> p (n t)"),
+            )
 
         def second_layer(t, cols, on_vector):
             bank = psum.tile([P, cols.stop - cols.start], F32, name="y_bank", tag="a" if t == 0 else "b")
             nc.tensor.matmul_mx(
                 out=bank[:],
-                lhsT=w2_codes[:, t, :].bitcast(FP8X4),
+                lhsT=w2_codes[t].bitcast(FP8X4),
                 lhsT_scale=w2_sc[t],
                 rhs=h_codes[:, cols].bitcast(FP8X4),
                 rhs_scale=h_sc[:, cols],
@@ -157,46 +195,32 @@ def tile_picked_zappnp_none_po_kernel(
             else:
                 nc.scalar.activation(out=y[t][:, cols], in_=bank[:], func=COPY, scale=0.2)
 
-        h_bf = [
-            keep.tile([P, b - a, PACK], BF16, name="h_bf", tag="h_bf%d" % i, align_bytes=64)
-            for i, (a, b) in enumerate(PIECES)
-        ]
-        for i, (a, b) in enumerate(PIECES):
-            for first in range(a, b, CHUNK):
-                cols = slice(first, first + CHUNK)
-                bank = psum.tile([P, PACK, CHUNK], F32, name="h_bank", tag="a" if first < HALF else "b")
-                for t in range(PACK):
-                    nc.tensor.matmul_mx(
-                        out=bank[:, t, :],
-                        lhsT=w1_codes[:, t * P : (t + 1) * P].bitcast(FP8X4),
-                        lhsT_scale=w1_sc[:, t * P : (t + 1) * P],
-                        rhs=x_codes[:, cols].bitcast(FP8X4),
-                        rhs_scale=x_sc[:, cols],
-                        start=True,
-                        stop=True,
-                    )
-                dst = h_bf[i][:, first - a : first - a + CHUNK, :]
-                src = bank[:].rearrange("p t n -> p n t")
-                if first // CHUNK in VECTOR_CHUNKS:
-                    nc.vector.tensor_copy(out=dst, in_=src)
-                else:
-                    nc.scalar.copy(out=dst, in_=src)
-        for i, (a, b) in enumerate(PIECES):
-            cols = slice(a, b)
-            nc.vector.quantize_mx(
-                out=h_codes[:, cols].bitcast(FP8X4),
-                scales=h_sc[:, cols],
-                in_=h_bf[i][:].rearrange("p n t -> p (n t)"),
-            )
-        for i, (a, b) in enumerate(PIECES):
-            second_layer(0, slice(a, b), i == 1)
-        w2_sc_rest = keep.tile([P, PACK - 1, P], U8, tag="h_bf%d" % (len(PIECES) - 1), align_bytes=64)
+        for chunk in range(S // CHUNK):
+            first_layer(chunk)
+
+        w2_word_view = w2_raw[:].rearrange("p (m t) -> p m t", t=PACK)
+        w2_scale_view = w2_scale_rows[:].rearrange("p (m t) -> p m t", t=PACK)
+        w2_codes_first = keep.tile([P, P], I32, tag="x_table", align_bytes=64)
+        nc.vector.tensor_copy(out=w2_codes_first[:], in_=w2_word_view[:, :, 0])
+        w2_sc_first = keep.tile([P, P], U8, tag="w1_bf1_0", align_bytes=64)
+        nc.vector.tensor_copy(out=w2_sc_first[:], in_=w2_scale_view[:, :, 0])
+        w2_codes = [w2_codes_first[:]]
+        w2_sc = [w2_sc_first[:]]
+
+        for piece in PIECE_ORDER:
+            quantise_hidden(piece)
+        for piece in PIECE_ORDER:
+            second_layer(0, slice(*PIECES[piece]), piece in VECTOR_PIECES)
+        last_piece = "h_bf%d" % PIECE_ORDER[-1]
+        w2_codes_rest = keep.tile([P, PACK - 1, P], I32, tag=last_piece, align_bytes=64)
+        nc.vector.tensor_copy(out=w2_codes_rest[:].rearrange("p t m -> p m t"), in_=w2_word_view[:, :, 1:])
+        w2_sc_rest = keep.tile([P, PACK - 1, P], U8, tag="h_bf%d" % PIECE_ORDER[-2], align_bytes=64)
         nc.vector.tensor_copy(out=w2_sc_rest[:].rearrange("p t m -> p m t"), in_=w2_scale_view[:, :, 1:])
+        w2_codes.extend(w2_codes_rest[:, t, :] for t in range(PACK - 1))
         w2_sc.extend(w2_sc_rest[:, t, :] for t in range(PACK - 1))
         for t in range(1, PACK):
             for u in range(2):
                 second_layer(t, slice(u * HALF, (u + 1) * HALF), False)
-
 
         def sum_on_tensor(terms, width, scale, dst, tag):
             blocks = [slice(b * P, (b + 1) * P) for b in range(width // P)]

@@ -26,7 +26,7 @@ PIECE_ORDER = (0, 1, 2, 3)
 VECTOR_CHUNKS = (3, 6)
 VECTOR_PIECES = (1,)
 WARM = 3
-FIRST_WORDS = 1536
+FIRST_WORDS = 1280
 
 
 def tile_picked_zappnp_none_po_kernel(
@@ -66,7 +66,9 @@ def tile_picked_zappnp_none_po_kernel(
         x_word_rows = x_words[0].rearrange("p c r -> p (c r)").bitcast(I32)
         nc.sync.dma_start(out=x_word_table[:, :FIRST_WORDS].bitcast(I32), in_=x_word_rows[:, :FIRST_WORDS])
         offs_t = load_list("offs_t", offs)
-        load_scale_rows(x_scale_table, x_scales, nc.sync)
+        pos_t = [load_list("pos%d_t" % d, src) for d, src in enumerate((pos1, pos2, pos3))]
+        cen_t = load_list("cen_t", cen)
+        nc.sync.dma_start(out=x_scale_table[4:P:8, :].bitcast(I32), in_=x_scales[0].bitcast(I32))
         nc.sync.dma_start(out=x_word_table[:, FIRST_WORDS:].bitcast(I32), in_=x_word_rows[:, FIRST_WORDS:])
         w1_raw = [load_w1_half(half) for half in range(2)]
         w2_scale_rows = keep.tile([P, N], U8, align_bytes=64)
@@ -74,8 +76,6 @@ def tile_picked_zappnp_none_po_kernel(
         w2_raw = keep.tile([P, N], I32, tag="w2_raw", align_bytes=64)
         nc.sync.dma_start(out=w2_raw[:], in_=w2_words[0].rearrange("p c r -> p (c r)").bitcast(I32))
         load_scale_rows(w2_scale_rows, w2_scales, nc.sync)
-        pos_t = [load_list("pos%d_t" % d, src) for d, src in enumerate((pos1, pos2, pos3))]
-        cen_t = load_list("cen_t", cen)
         gate_t = keep.tile([P, D, V], F32, align_bytes=64)
         nc.sync.dma_start(out=gate_t[:], in_=gate.rearrange("d p v -> p d v"))
         nxt_t = [load_list("nxt%d_t" % d, src) for d, src in enumerate((nxt1, nxt2, nxt3))]
@@ -86,8 +86,10 @@ def tile_picked_zappnp_none_po_kernel(
         identity = keep.tile([P, P], F32, align_bytes=64)
         make_identity(nc, identity[:])
 
+        ones = keep.tile([P, V], F32, align_bytes=64)
+        nc.gpsimd.memset(ones[:], 1.0)
         quarter = keep.tile([P, V], F32, align_bytes=64)
-        nc.gpsimd.memset(quarter[:], 0.25)
+        nc.scalar.activation(out=quarter[:], in_=ones[:], func=COPY, scale=0.25)
 
         w1_codes = keep.tile([P, H], U32, align_bytes=64)
         w1_sc = keep.tile([P, H], U8, align_bytes=64)
@@ -121,17 +123,23 @@ def tile_picked_zappnp_none_po_kernel(
             )
             return codes
 
+        x_sc_spread = keep.tile([P, S], U8, align_bytes=64)
+        nc.vector.tensor_copy(x_sc_spread[:], x_scale_table[:].indirect(offs_t[:]))
         x_sc = keep.tile([P, S], U8, align_bytes=64)
-        nc.vector.tensor_copy(x_sc[:], x_scale_table[:].indirect(offs_t[:]))
+        nc.gpsimd.memset(x_sc[:].bitcast(I32), 0)
+        for r in range(4):
+            nc.scalar.dma_start(
+                out=x_sc[r:P:32, :].bitcast(I32), in_=x_sc_spread[8 * r + 4 : P : 32, :].bitcast(I32)
+            )
         x_codes = [gather_words(0, "x_bytes")]
         for t in range(WARM):
             warm = psum.tile([P, HALF], F32, name="warm", tag="b")
             nc.tensor.matmul_mx(
                 out=warm[:],
                 lhsT=x_codes[0][:, t * P : (t + 1) * P].bitcast(FP8X4),
-                lhsT_scale=x_sc[:, t * P : (t + 1) * P],
+                lhsT_scale=x_sc_spread[:, t * P : (t + 1) * P],
                 rhs=x_codes[0][:].bitcast(FP8X4),
-                rhs_scale=x_sc[:, :HALF],
+                rhs_scale=x_sc_spread[:, :HALF],
                 start=True,
                 stop=True,
             )

@@ -23,8 +23,8 @@ HALF = S // 2
 CHUNK = 128
 PIECES = ((0, 512), (512, 768), (768, 896), (896, 1024))
 PIECE_ORDER = (0, 1, 2, 3)
-VECTOR_CHUNKS = (3, 6)
-VECTOR_PIECES = (1,)
+VECTOR_CHUNKS = (3, 4)
+Y_PIECES = PIECES
 WARM = 3
 FIRST_WORDS = 1280
 
@@ -60,22 +60,22 @@ def tile_picked_zappnp_none_po_kernel(
             )
             return part
 
+        w2_scale_rows = keep.tile([P, N], U8, align_bytes=64)
+        nc.gpsimd.memset(w2_scale_rows[:].bitcast(I32), 0)
         x_scale_table = keep.tile([P, T], U8, tag="x_bytes", align_bytes=64)
         nc.gpsimd.memset(x_scale_table[:].bitcast(I32), 0)
         x_word_table = keep.tile([P, T], U32, tag="x_table", align_bytes=64)
         x_word_rows = x_words[0].rearrange("p c r -> p (c r)").bitcast(I32)
         nc.sync.dma_start(out=x_word_table[:, :FIRST_WORDS].bitcast(I32), in_=x_word_rows[:, :FIRST_WORDS])
         offs_t = load_list("offs_t", offs)
-        pos_t = [load_list("pos%d_t" % d, src) for d, src in enumerate((pos1, pos2, pos3))]
-        cen_t = load_list("cen_t", cen)
+        load_scale_rows(w2_scale_rows, w2_scales, nc.sync)
         nc.sync.dma_start(out=x_scale_table[4:P:8, :].bitcast(I32), in_=x_scales[0].bitcast(I32))
         nc.sync.dma_start(out=x_word_table[:, FIRST_WORDS:].bitcast(I32), in_=x_word_rows[:, FIRST_WORDS:])
         w1_raw = [load_w1_half(half) for half in range(2)]
-        w2_scale_rows = keep.tile([P, N], U8, align_bytes=64)
-        nc.gpsimd.memset(w2_scale_rows[:].bitcast(I32), 0)
         w2_raw = keep.tile([P, N], I32, tag="w2_raw", align_bytes=64)
         nc.sync.dma_start(out=w2_raw[:], in_=w2_words[0].rearrange("p c r -> p (c r)").bitcast(I32))
-        load_scale_rows(w2_scale_rows, w2_scales, nc.sync)
+        pos_t = [load_list("pos%d_t" % d, src) for d, src in enumerate((pos1, pos2, pos3))]
+        cen_t = load_list("cen_t", cen)
         gate_t = keep.tile([P, D, V], F32, align_bytes=64)
         nc.sync.dma_start(out=gate_t[:], in_=gate.rearrange("d p v -> p d v"))
         nxt_t = [load_list("nxt%d_t" % d, src) for d, src in enumerate((nxt1, nxt2, nxt3))]
@@ -131,6 +131,12 @@ def tile_picked_zappnp_none_po_kernel(
             nc.scalar.dma_start(
                 out=x_sc[r:P:32, :].bitcast(I32), in_=x_sc_spread[8 * r + 4 : P : 32, :].bitcast(I32)
             )
+        w2_sc_dealt = keep.tile([P, PACK, P], U8, align_bytes=64)
+        nc.vector.tensor_copy(
+            out=w2_sc_dealt[:].rearrange("p t m -> p m t"),
+            in_=w2_scale_rows[:].rearrange("p (m t) -> p m t", t=PACK),
+        )
+        w2_sc = [w2_sc_dealt[:, t, :] for t in range(PACK)]
         x_codes = [gather_words(0, "x_bytes")]
         for t in range(WARM):
             warm = psum.tile([P, HALF], F32, name="warm", tag="b")
@@ -157,24 +163,26 @@ def tile_picked_zappnp_none_po_kernel(
             for i, (a, b) in enumerate(PIECES)
         ]
 
-        def first_layer(chunk):
-            first = chunk * CHUNK
-            piece = max(i for i, (a, b) in enumerate(PIECES) if a <= first)
-            within = first - PIECES[piece][0]
-            bank = psum.tile([P, PACK, CHUNK], F32, name="h_bank", tag="a" if first < HALF else "b")
+        def first_layer(first, width, tag):
+            bank = psum.tile([P, PACK, width], F32, name="h_bank", tag=tag)
             for t in reversed(range(PACK)):
                 nc.tensor.matmul_mx(
                     out=bank[:, t, :],
                     lhsT=w1_codes[:, t * P : (t + 1) * P].bitcast(FP8X4),
                     lhsT_scale=w1_sc[:, t * P : (t + 1) * P],
-                    rhs=x_codes[first // HALF][:, first % HALF : first % HALF + CHUNK].bitcast(FP8X4),
-                    rhs_scale=x_sc[:, first : first + CHUNK],
+                    rhs=x_codes[first // HALF][:, first % HALF : first % HALF + width].bitcast(FP8X4),
+                    rhs_scale=x_sc[:, first : first + width],
                     start=True,
                     stop=True,
                 )
-            dst = h_bf[piece][:, within : within + CHUNK, :]
+            return bank
+
+        def round_hidden(bank, first, width, on_vector):
+            piece = max(i for i, (a, b) in enumerate(PIECES) if a <= first)
+            within = first - PIECES[piece][0]
+            dst = h_bf[piece][:, within : within + width, :]
             src = bank[:].rearrange("p t n -> p n t")
-            if chunk in VECTOR_CHUNKS:
+            if on_vector:
                 nc.vector.tensor_copy(out=dst, in_=src)
             else:
                 nc.scalar.copy(out=dst, in_=src)
@@ -203,29 +211,28 @@ def tile_picked_zappnp_none_po_kernel(
             else:
                 nc.scalar.activation(out=y[t][:, cols], in_=bank[:], func=COPY, scale=0.2)
 
-        for chunk in range(S // CHUNK):
-            first_layer(chunk)
+        for chunk in range(S // CHUNK - 1):
+            first = chunk * CHUNK
+            bank = first_layer(first, CHUNK, "a" if first < HALF else "b")
+            round_hidden(bank, first, CHUNK, chunk in VECTOR_CHUNKS)
+        tail_bank = first_layer(S - CHUNK // 2, CHUNK // 2, "b")
+        round_hidden(first_layer(S - CHUNK, CHUNK // 2, "a"), S - CHUNK, CHUNK // 2, False)
 
         w2_word_view = w2_raw[:].rearrange("p (m t) -> p m t", t=PACK)
-        w2_scale_view = w2_scale_rows[:].rearrange("p (m t) -> p m t", t=PACK)
         w2_codes_first = keep.tile([P, P], I32, tag="x_table", align_bytes=64)
         nc.vector.tensor_copy(out=w2_codes_first[:], in_=w2_word_view[:, :, 0])
-        w2_sc_first = keep.tile([P, P], U8, tag="w1_bf1_0", align_bytes=64)
-        nc.vector.tensor_copy(out=w2_sc_first[:], in_=w2_scale_view[:, :, 0])
         w2_codes = [w2_codes_first[:]]
-        w2_sc = [w2_sc_first[:]]
 
-        for piece in PIECE_ORDER:
+        quantise_hidden(0)
+        round_hidden(tail_bank, S - CHUNK // 2, CHUNK // 2, True)
+        for piece in PIECE_ORDER[1:]:
             quantise_hidden(piece)
-        for piece in PIECE_ORDER:
-            second_layer(0, slice(*PIECES[piece]), piece in VECTOR_PIECES)
+        for a, b in Y_PIECES:
+            second_layer(0, slice(a, b), a == 768)
         last_piece = "h_bf%d" % PIECE_ORDER[-1]
         w2_codes_rest = keep.tile([P, PACK - 1, P], I32, tag=last_piece, align_bytes=64)
         nc.vector.tensor_copy(out=w2_codes_rest[:].rearrange("p t m -> p m t"), in_=w2_word_view[:, :, 1:])
-        w2_sc_rest = keep.tile([P, PACK - 1, P], U8, tag="h_bf%d" % PIECE_ORDER[-2], align_bytes=64)
-        nc.vector.tensor_copy(out=w2_sc_rest[:].rearrange("p t m -> p m t"), in_=w2_scale_view[:, :, 1:])
         w2_codes.extend(w2_codes_rest[:, t, :] for t in range(PACK - 1))
-        w2_sc.extend(w2_sc_rest[:, t, :] for t in range(PACK - 1))
         for t in range(1, PACK):
             for u in range(2):
                 second_layer(t, slice(u * HALF, (u + 1) * HALF), False)
@@ -264,14 +271,15 @@ def tile_picked_zappnp_none_po_kernel(
         mixed2 = [keep.tile([P, U], F32, name="mixed2_%d" % t, align_bytes=64) for t in range(PACK)]
         halves = [slice(0, U // 2), slice(U // 2, U)]
 
-        def neighbours_2(t, cols, tag):
-            for d in range(D):
-                nc.vector.tensor_tensor(
-                    far[:, t, d, cols],
-                    z[t][:].indirect(nxt_t[d][:, cols.start // 16 : cols.stop // 16]),
-                    gate2_t[:, d, cols],
-                    MULT,
-                )
+        def gather_far(t, d, cols):
+            nc.vector.tensor_tensor(
+                far[:, t, d, cols],
+                z[t][:].indirect(nxt_t[d][:, cols.start // 16 : cols.stop // 16]),
+                gate2_t[:, d, cols],
+                MULT,
+            )
+
+        def sum_far(t, cols, tag):
             terms = [far[:, t, d, cols] for d in range(D)]
             sum_on_tensor(terms, cols.stop - cols.start, 1.0, mixed2[t][:, cols], tag)
 
@@ -290,9 +298,14 @@ def tile_picked_zappnp_none_po_kernel(
         nc.scalar.activation(out=gate2_t[:], in_=gate2_raw[:], func=COPY, scale=0.8)
         far = keep.tile([P, PACK, D, U], F32, name="far", align_bytes=64)
         for t in range(last):
-            neighbours_2(t, slice(0, U), "turned_sb")
-        neighbours_2(last, halves[0], "turned_sb")
-        neighbours_2(last, halves[1], "last_turned")
+            for d in range(D):
+                gather_far(t, d, slice(0, U))
+            sum_far(t, slice(0, U), "turned_sb")
+        for d in range(D - 1):
+            gather_far(last, d, slice(0, U))
+        for cols, tag in zip(halves, ("turned_sb", "last_turned")):
+            gather_far(last, D - 1, cols)
+            sum_far(last, cols, tag)
 
         result = keep.tile([P, PACK, U], F32, name="result", tag="near0_0", align_bytes=64)
         for t in range(last):

@@ -25,7 +25,7 @@ PIECES = ((0, 512), (512, 768), (768, 896), (896, 1024))
 PIECE_ORDER = (0, 1, 2, 3)
 VECTOR_CHUNKS = (3, 4)
 Y_PIECES = PIECES
-WARM = 3
+WARM = 2
 FIRST_WORDS = 1280
 
 
@@ -153,7 +153,7 @@ def tile_picked_zappnp_none_po_kernel(
             late = [round_w1(half, u, u == 0) for u in range(2)]
             for u in range(2):
                 quantise_w1(half, u, late[u])
-        x_codes.append(gather_words(1, "w1_bf1_1"))
+        x_codes.append(gather_words(1, "w1_raw1"))
 
         h_codes = keep.tile([P, S], U32, align_bytes=64)
         h_sc = keep.tile([P, S], U8, align_bytes=64)
@@ -165,7 +165,7 @@ def tile_picked_zappnp_none_po_kernel(
 
         def first_layer(first, width, tag):
             bank = psum.tile([P, PACK, width], F32, name="h_bank", tag=tag)
-            for t in reversed(range(PACK)):
+            for t in range(PACK) if first == 0 else reversed(range(PACK)):
                 nc.tensor.matmul_mx(
                     out=bank[:, t, :],
                     lhsT=w1_codes[:, t * P : (t + 1) * P].bitcast(FP8X4),
@@ -219,7 +219,7 @@ def tile_picked_zappnp_none_po_kernel(
         round_hidden(first_layer(S - CHUNK, CHUNK // 2, "a"), S - CHUNK, CHUNK // 2, False)
 
         w2_word_view = w2_raw[:].rearrange("p (m t) -> p m t", t=PACK)
-        w2_codes_first = keep.tile([P, P], I32, tag="x_table", align_bytes=64)
+        w2_codes_first = keep.tile([P, P], I32, tag="w1_bf1_1", align_bytes=64)
         nc.vector.tensor_copy(out=w2_codes_first[:], in_=w2_word_view[:, :, 0])
         w2_codes = [w2_codes_first[:]]
 
@@ -228,7 +228,7 @@ def tile_picked_zappnp_none_po_kernel(
         for piece in PIECE_ORDER[1:]:
             quantise_hidden(piece)
         for a, b in Y_PIECES:
-            second_layer(0, slice(a, b), a == 768)
+            second_layer(0, slice(a, b), a == 512)
         last_piece = "h_bf%d" % PIECE_ORDER[-1]
         w2_codes_rest = keep.tile([P, PACK - 1, P], I32, tag=last_piece, align_bytes=64)
         nc.vector.tensor_copy(out=w2_codes_rest[:].rearrange("p t m -> p m t"), in_=w2_word_view[:, :, 1:])

@@ -26,6 +26,7 @@ PIECE_ORDER = (0, 1, 2, 3)
 VECTOR_CHUNKS = (3, 4)
 Y_PIECES = PIECES
 WARM = 2
+SCALAR_ROWS = 48
 FIRST_WORDS = 1280
 
 
@@ -94,16 +95,16 @@ def tile_picked_zappnp_none_po_kernel(
         w1_codes = keep.tile([P, H], U32, align_bytes=64)
         w1_sc = keep.tile([P, H], U8, align_bytes=64)
 
-        def round_w1(half, u, on_vector):
-            dealt = keep.tile(
-                [P, 2, P // 2, PACK], BF16, name="w1_bf", tag="w1_bf%d_%d" % (half, u), align_bytes=64
-            )
-            dst = dealt[:].rearrange("p t m j -> p m t j")
-            src = w1_raw[half][:].rearrange("p j (m t) -> p m t j", t=PACK)[:, :, 2 * u : 2 * u + 2, :]
-            if on_vector:
-                nc.vector.tensor_copy(out=dst, in_=src)
-            else:
-                nc.scalar.activation(out=dst, in_=src, func=COPY)
+        def round_w1(half):
+            dealt = [
+                keep.tile([P, 2, P // 2, PACK], BF16, name="w1_bf", tag="w1_bf%d_%d" % (half, u), align_bytes=64)
+                for u in range(2)
+            ]
+            dst = [tile[:].rearrange("p t m j -> p m t j") for tile in dealt]
+            src = w1_raw[half][:].rearrange("p j (m t) -> p m t j", t=PACK)
+            nc.scalar.activation(out=dst[1][:, :SCALAR_ROWS], in_=src[:, :SCALAR_ROWS, 2:, :], func=COPY)
+            nc.vector.tensor_copy(out=dst[0], in_=src[:, :, :2, :])
+            nc.vector.tensor_copy(out=dst[1][:, SCALAR_ROWS:], in_=src[:, SCALAR_ROWS:, 2:, :])
             return dealt
 
         def quantise_w1(half, u, dealt):
@@ -150,7 +151,7 @@ def tile_picked_zappnp_none_po_kernel(
                 stop=True,
             )
         for half in range(2):
-            late = [round_w1(half, u, u == 0) for u in range(2)]
+            late = round_w1(half)
             for u in range(2):
                 quantise_w1(half, u, late[u])
         x_codes.append(gather_words(1, "w1_raw1"))

@@ -62,9 +62,9 @@ def tile_picked_zappnp_none_po_kernel(
             return part
 
         w2_scale_rows = keep.tile([P, N], U8, align_bytes=64)
-        nc.gpsimd.memset(w2_scale_rows[:].bitcast(I32), 0)
+        nc.vector.memset(w2_scale_rows[:].bitcast(I32), 0)
         x_scale_table = keep.tile([P, T], U8, tag="x_bytes", align_bytes=64)
-        nc.gpsimd.memset(x_scale_table[:].bitcast(I32), 0)
+        nc.vector.memset(x_scale_table[:].bitcast(I32), 0)
         x_word_table = keep.tile([P, T], U32, tag="x_table", align_bytes=64)
         x_word_rows = x_words[0].rearrange("p c r -> p (c r)").bitcast(I32)
         nc.sync.dma_start(out=x_word_table[:, :FIRST_WORDS].bitcast(I32), in_=x_word_rows[:, :FIRST_WORDS])
@@ -88,7 +88,7 @@ def tile_picked_zappnp_none_po_kernel(
         make_identity(nc, identity[:])
 
         ones = keep.tile([P, V], F32, align_bytes=64)
-        nc.gpsimd.memset(ones[:], 1.0)
+        nc.vector.memset(ones[:], 1.0)
         quarter = keep.tile([P, V], F32, align_bytes=64)
         nc.scalar.activation(out=quarter[:], in_=ones[:], func=COPY, scale=0.25)
 
@@ -127,7 +127,7 @@ def tile_picked_zappnp_none_po_kernel(
         x_sc_spread = keep.tile([P, S], U8, align_bytes=64)
         nc.vector.tensor_copy(x_sc_spread[:], x_scale_table[:].indirect(offs_t[:]))
         x_sc = keep.tile([P, S], U8, align_bytes=64)
-        nc.gpsimd.memset(x_sc[:].bitcast(I32), 0)
+        nc.vector.memset(x_sc[:].bitcast(I32), 0)
         for r in range(4):
             nc.scalar.dma_start(
                 out=x_sc[r:P:32, :].bitcast(I32), in_=x_sc_spread[8 * r + 4 : P : 32, :].bitcast(I32)

@@ -53,11 +53,11 @@ def tile_picked_zappnp_none_po_kernel(
                     in_=source[0, r:16:4, :].bitcast(I32),
                 )
 
-        def load_w1_half(half):
-            part = keep.tile([P, PACK, H // 2], F32, name="w1_raw%d" % half, align_bytes=64)
+        def load_w1(half, j0, j1):
+            part = keep.tile([P, j1 - j0, H // 2], F32, name="w1_raw%d_%d" % (half, j0), align_bytes=64)
             nc.sync.dma_start(
                 out=part[:],
-                in_=w1.rearrange("(p j) c -> p j c", j=PACK)[:, :, half * H // 2 : (half + 1) * H // 2],
+                in_=w1.rearrange("(p j) c -> p j c", j=PACK)[:, j0:j1, half * H // 2 : (half + 1) * H // 2],
             )
             return part
 
@@ -72,7 +72,8 @@ def tile_picked_zappnp_none_po_kernel(
         load_scale_rows(w2_scale_rows, w2_scales, nc.sync)
         nc.sync.dma_start(out=x_scale_table[4:P:8, :].bitcast(I32), in_=x_scales[0].bitcast(I32))
         nc.sync.dma_start(out=x_word_table[:, FIRST_WORDS:].bitcast(I32), in_=x_word_rows[:, FIRST_WORDS:])
-        w1_raw = [load_w1_half(half) for half in range(2)]
+        w1_raw = load_w1(0, 0, PACK)
+        w1_late = [load_w1(1, j, j + 2) for j in (0, 2)]
         w2_raw = keep.tile([P, N], I32, tag="w2_raw", align_bytes=64)
         nc.sync.dma_start(out=w2_raw[:], in_=w2_words[0].rearrange("p c r -> p (c r)").bitcast(I32))
         pos_t = [load_list("pos%d_t" % d, src) for d, src in enumerate((pos1, pos2, pos3))]
@@ -101,10 +102,17 @@ def tile_picked_zappnp_none_po_kernel(
                 for u in range(2)
             ]
             dst = [tile[:].rearrange("p t m j -> p m t j") for tile in dealt]
-            src = w1_raw[half][:].rearrange("p j (m t) -> p m t j", t=PACK)
-            nc.scalar.activation(out=dst[1][:, :SCALAR_ROWS], in_=src[:, :SCALAR_ROWS, 2:, :], func=COPY)
-            nc.vector.tensor_copy(out=dst[0], in_=src[:, :, :2, :])
-            nc.vector.tensor_copy(out=dst[1][:, SCALAR_ROWS:], in_=src[:, SCALAR_ROWS:, 2:, :])
+            if half == 0:
+                src = w1_raw[:].rearrange("p j (m t) -> p m t j", t=PACK)
+                nc.scalar.activation(out=dst[1][:, :SCALAR_ROWS], in_=src[:, :SCALAR_ROWS, 2:, :], func=COPY)
+                nc.vector.tensor_copy(out=dst[0], in_=src[:, :, :2, :])
+                nc.vector.tensor_copy(out=dst[1][:, SCALAR_ROWS:], in_=src[:, SCALAR_ROWS:, 2:, :])
+                return dealt
+            for pair, part in enumerate(w1_late):
+                src = part[:].rearrange("p j (m t) -> p m t j", t=PACK)
+                rows = slice(2 * pair, 2 * pair + 2)
+                nc.scalar.activation(out=dst[1][:, :, :, rows], in_=src[:, :, 2:, :], func=COPY)
+                nc.vector.tensor_copy(out=dst[0][:, :, :, rows], in_=src[:, :, :2, :])
             return dealt
 
         def quantise_w1(half, u, dealt):
@@ -154,7 +162,7 @@ def tile_picked_zappnp_none_po_kernel(
             late = round_w1(half)
             for u in range(2):
                 quantise_w1(half, u, late[u])
-        x_codes.append(gather_words(1, "w1_raw1"))
+        x_codes.append(gather_words(1, "w1_raw1_2"))
 
         h_codes = keep.tile([P, S], U32, align_bytes=64)
         h_sc = keep.tile([P, S], U8, align_bytes=64)

@@ -23,9 +23,9 @@ HALF = S // 2
 CHUNK = 128
 PIECES = ((0, 512), (512, 768), (768, 896), (896, 1024))
 PIECE_ORDER = (0, 1, 2, 3)
-VECTOR_CHUNKS = (3, 4)
+VECTOR_CHUNKS = (2, 4)
 Y_PIECES = PIECES
-WARM = 2
+WARM = 3
 SCALAR_ROWS = 48
 FIRST_WORDS = 1280
 

@@ -282,14 +282,14 @@ def tile_picked_zappnp_none_po_kernel(
 
         def gather_far(t, d, cols):
             nc.vector.tensor_tensor(
-                far[:, t, d, cols],
+                far[t][:, d, cols],
                 z[t][:].indirect(nxt_t[d][:, cols.start // 16 : cols.stop // 16]),
                 gate2_t[:, d, cols],
                 MULT,
             )
 
         def sum_far(t, cols, tag):
-            terms = [far[:, t, d, cols] for d in range(D)]
+            terms = [far[t][:, d, cols] for d in range(D)]
             sum_on_tensor(terms, cols.stop - cols.start, 1.0, mixed2[t][:, cols], tag)
 
         def restart_2(t, cols):
@@ -305,18 +305,18 @@ def tile_picked_zappnp_none_po_kernel(
             neighbours_1(t)
         gate2_t = keep.tile([P, D, U], F32, name="gate2_t", tag="near0_0", align_bytes=64)
         nc.scalar.activation(out=gate2_t[:], in_=gate2_raw[:], func=COPY, scale=0.8)
-        far = keep.tile([P, PACK, D, U], F32, name="far", align_bytes=64)
+        far = [keep.tile([P, D, U], F32, name="far", tag="far%d" % t, align_bytes=64) for t in range(PACK)]
         for t in range(last):
             for d in range(D):
                 gather_far(t, d, slice(0, U))
             sum_far(t, slice(0, U), "turned_sb")
-        for d in range(D - 1):
-            gather_far(last, d, slice(0, U))
+        gather_far(last, 0, slice(0, U))
         for cols, tag in zip(halves, ("turned_sb", "last_turned")):
-            gather_far(last, D - 1, cols)
+            for d in range(1, D):
+                gather_far(last, d, cols)
             sum_far(last, cols, tag)
 
-        result = keep.tile([P, PACK, U], F32, name="result", tag="near0_0", align_bytes=64)
+        result = keep.tile([P, PACK, U], F32, name="result", tag="far2", align_bytes=64)
         for t in range(last):
             restart_2(t, slice(0, U))
             nc.sync.dma_start(out=out_rows[:, t, :], in_=result[:, t, :])

@@ -27,6 +27,7 @@ VECTOR_CHUNKS = (2, 4)
 Y_PIECES = PIECES
 WARM = 3
 SCALAR_ROWS = 48
+LAST_SCALAR_ROWS = 32
 FIRST_WORDS = 1280
 
 
@@ -111,8 +112,11 @@ def tile_picked_zappnp_none_po_kernel(
             for pair, part in enumerate(w1_late):
                 src = part[:].rearrange("p j (m t) -> p m t j", t=PACK)
                 rows = slice(2 * pair, 2 * pair + 2)
-                nc.scalar.activation(out=dst[1][:, :, :, rows], in_=src[:, :, 2:, :], func=COPY)
+                split = LAST_SCALAR_ROWS if pair else P // 2
+                nc.scalar.activation(out=dst[1][:, :split, :, rows], in_=src[:, :split, 2:, :], func=COPY)
                 nc.vector.tensor_copy(out=dst[0][:, :, :, rows], in_=src[:, :, :2, :])
+                if pair:
+                    nc.vector.tensor_copy(out=dst[1][:, split:, :, rows], in_=src[:, split:, 2:, :])
             return dealt
 
         def quantise_w1(half, u, dealt):

@@ -40,7 +40,7 @@ def tile_picked_zappnp_none_po_kernel(
         lists = ctx.enter_context(tc.tile_pool(name="lists", bufs=1))
         keep = ctx.enter_context(tc.tile_pool(name="keep", bufs=1))
         ring = ctx.enter_context(tc.tile_pool(name="ring", bufs=2))
-        psum = ctx.enter_context(tc.psum_pool(name="psum", bufs=4))
+        psum = ctx.enter_context(tc.psum_pool(name="psum", bufs=1))
 
         def load_list(name, source):
             tile = lists.tile(list(source.shape), U16, name=name)
@@ -86,13 +86,11 @@ def tile_picked_zappnp_none_po_kernel(
         gate2_raw = keep.tile([P, D, U], F32, align_bytes=64)
         nc.sync.dma_start(out=gate2_raw[:], in_=gate2.rearrange("d p x -> p d x"))
 
+        zero = keep.tile([P, 1], F32, align_bytes=64)
+        nc.vector.memset(zero[:], 0.0)
         identity = keep.tile([P, P], F32, align_bytes=64)
-        make_identity(nc, identity[:])
-
-        ones = keep.tile([P, V], F32, align_bytes=64)
-        nc.vector.memset(ones[:], 1.0)
-        quarter = keep.tile([P, V], F32, align_bytes=64)
-        nc.scalar.activation(out=quarter[:], in_=ones[:], func=COPY, scale=0.25)
+        nc.scalar.activation(out=identity[:], in_=zero[:].to_broadcast([P, P]), func=COPY)
+        make_identity(nc, identity[:], nomemset=True)
 
         w1_codes = keep.tile([P, H], U32, align_bytes=64)
         w1_sc = keep.tile([P, H], U8, align_bytes=64)
@@ -152,7 +150,7 @@ def tile_picked_zappnp_none_po_kernel(
         w2_sc = [w2_sc_dealt[:, t, :] for t in range(PACK)]
         x_codes = [gather_words(0, "x_bytes")]
         for t in range(WARM):
-            warm = psum.tile([P, HALF], F32, name="warm", tag="b")
+            warm = psum.tile([P, HALF], F32, name="warm", tag="bank%d" % (4 + t))
             nc.tensor.matmul_mx(
                 out=warm[:],
                 lhsT=x_codes[0][:, t * P : (t + 1) * P].bitcast(FP8X4),
@@ -208,8 +206,8 @@ def tile_picked_zappnp_none_po_kernel(
                 in_=h_bf[piece][:].rearrange("p n t -> p (n t)"),
             )
 
-        def second_layer(t, cols, on_vector):
-            bank = psum.tile([P, cols.stop - cols.start], F32, name="y_bank", tag="a" if t == 0 else "b")
+        def second_layer(t, cols, on_vector, tag):
+            bank = psum.tile([P, cols.stop - cols.start], F32, name="y_bank", tag=tag)
             nc.tensor.matmul_mx(
                 out=bank[:],
                 lhsT=w2_codes[t].bitcast(FP8X4),
@@ -220,16 +218,16 @@ def tile_picked_zappnp_none_po_kernel(
                 stop=True,
             )
             if on_vector:
-                nc.vector.tensor_scalar_mul(y[t][:, cols], bank[:], 0.2)
+                nc.vector.tensor_copy(out=y[t][:, cols], in_=bank[:])
             else:
-                nc.scalar.activation(out=y[t][:, cols], in_=bank[:], func=COPY, scale=0.2)
+                nc.scalar.copy(out=y[t][:, cols], in_=bank[:])
 
         for chunk in range(S // CHUNK - 1):
             first = chunk * CHUNK
-            bank = first_layer(first, CHUNK, "a" if first < HALF else "b")
+            bank = first_layer(first, CHUNK, "bank%d" % chunk)
             round_hidden(bank, first, CHUNK, chunk in VECTOR_CHUNKS)
-        tail_bank = first_layer(S - CHUNK // 2, CHUNK // 2, "b")
-        round_hidden(first_layer(S - CHUNK, CHUNK // 2, "a"), S - CHUNK, CHUNK // 2, False)
+        tail_bank = first_layer(S - CHUNK // 2, CHUNK // 2, "bank7")
+        round_hidden(first_layer(S - CHUNK, CHUNK // 2, "bank0"), S - CHUNK, CHUNK // 2, False)
 
         w2_word_view = w2_raw[:].rearrange("p (m t) -> p m t", t=PACK)
         w2_codes_first = keep.tile([P, P], I32, tag="w1_bf1_1", align_bytes=64)
@@ -240,99 +238,102 @@ def tile_picked_zappnp_none_po_kernel(
         round_hidden(tail_bank, S - CHUNK // 2, CHUNK // 2, True)
         for piece in PIECE_ORDER[1:]:
             quantise_hidden(piece)
-        for a, b in Y_PIECES:
-            second_layer(0, slice(a, b), a == 512)
+        for i, (a, b) in enumerate(Y_PIECES):
+            second_layer(0, slice(a, b), a == 512, "bank%d" % (1 + i))
         last_piece = "h_bf%d" % PIECE_ORDER[-1]
         w2_codes_rest = keep.tile([P, PACK - 1, P], I32, tag=last_piece, align_bytes=64)
         nc.vector.tensor_copy(out=w2_codes_rest[:].rearrange("p t m -> p m t"), in_=w2_word_view[:, :, 1:])
         w2_codes.extend(w2_codes_rest[:, t, :] for t in range(PACK - 1))
-        for t in range(1, PACK):
-            for u in range(2):
-                second_layer(t, slice(u * HALF, (u + 1) * HALF), False)
 
-        def sum_on_tensor(terms, width, scale, dst, tag):
+        def second_layer_tile(t):
+            for u in range(2):
+                second_layer(t, slice(u * HALF, (u + 1) * HALF), False, "bank%d" % ((3 + 2 * t + u) % 8))
+
+        def turn_and_add(terms, width, name, tag):
             blocks = [slice(b * P, (b + 1) * P) for b in range(width // P)]
-            banks = [psum.tile([P, P], F32, name="turned", tag="a") for cols in blocks]
+            turned = psum.tile([P, width], F32, name="turned", tag=tag)
             for i, term in enumerate(terms):
-                for bank, cols in zip(banks, blocks):
+                for b, cols in enumerate(blocks):
                     nc.tensor.matmul(
-                        bank[:], term[:, cols], identity[:],
-                        start=(i == 0), stop=(i == len(terms) - 1), is_transpose=True,
+                        turned[:, cols], term[:, cols], identity[:],
+                        start=(i == 0 and b == 0),
+                        stop=(i == len(terms) - 1 and b == len(blocks) - 1),
+                        is_transpose=True,
                     )
-            pool = ring if tag == "turned_sb" else keep
-            turned_sb = pool.tile([P, width], F32, name="turned_sb", tag=tag, align_bytes=64)
-            back = psum.tile([P, width], F32, name="back", tag="b")
-            for bank, cols in zip(banks, blocks):
-                nc.scalar.activation(out=turned_sb[:, cols], in_=bank[:], func=COPY, scale=scale)
-            for cols in blocks:
+            turned_sb = keep.tile([P, width], F32, name=name, align_bytes=64)
+            nc.scalar.activation(out=turned_sb[:], in_=turned[:], func=COPY, scale=0.8)
+            return turned_sb
+
+        def turn_back(turned_sb, width, tag):
+            back = psum.tile([P, width], F32, name="back", tag=tag)
+            for b in range(width // P):
+                cols = slice(b * P, (b + 1) * P)
                 nc.tensor.transpose(back[:, cols], turned_sb[:, cols], identity[:])
-            nc.scalar.copy(out=dst, in_=back[:])
+            return back
 
         z = [keep.tile([P, V], F32, name="z", tag="z%d" % t, align_bytes=64) for t in range(PACK)]
         out_rows = out_0.rearrange("(p t) x -> p t x", t=PACK)
+        result = keep.tile([P, PACK, U], F32, name="result", align_bytes=64)
 
-        def neighbours_1(t):
+        def gated_terms(t, window, near_lists, gates, width, tag):
             terms = []
-            for d in range(D):
-                term = keep.tile([P, V], F32, name="near", tag="near%d_%d" % (t, d), align_bytes=64)
-                nc.vector.tensor_tensor(term[:], y[t][:].indirect(pos_t[d][:]), gate_t[:, d, :], MULT)
+            for d, near in enumerate(near_lists):
+                term = keep.tile([P, width], F32, name="near", tag="%s%d_%d" % (tag, t, d), align_bytes=64)
+                nc.vector.tensor_tensor(term[:], window[:].indirect(near[:]), gates[:, d, :], MULT)
                 terms.append(term)
-            own = keep.tile([P, V], F32, name="own", tag="own%d" % t, align_bytes=64)
-            nc.vector.tensor_tensor(own[:], y[t][:].indirect(cen_t[:]), quarter[:], MULT)
-            sum_on_tensor(terms + [own], V, 4.0, z[t][:], "turned_sb")
+            return terms
 
-        mixed2 = [keep.tile([P, U], F32, name="mixed2_%d" % t, align_bytes=64) for t in range(PACK)]
-        halves = [slice(0, U // 2), slice(U // 2, U)]
+        def scalar_gather(dst, window, offsets, scale):
+            nc.scalar.activation(out=dst, in_=window[:].indirect(offsets[:]), func=COPY, scale=scale)
 
-        def gather_far(t, d, cols):
-            nc.vector.tensor_tensor(
-                far[t][:, d, cols],
-                z[t][:].indirect(nxt_t[d][:, cols.start // 16 : cols.stop // 16]),
-                gate2_t[:, d, cols],
-                MULT,
-            )
+        def centre_term(t):
+            own = ring.tile([P, V], F32, name="own", tag="own", align_bytes=64)
+            scalar_gather(own[:], y[t], cen_t, 0.25)
+            return own
 
-        def sum_far(t, cols, tag):
-            terms = [far[t][:, d, cols] for d in range(D)]
-            sum_on_tensor(terms, cols.stop - cols.start, 1.0, mixed2[t][:, cols], tag)
-
-        def restart_2(t, cols):
-            nc.vector.tensor_tensor(
-                result[:, t, cols],
-                y[t][:].indirect(root_t[:, cols.start // 16 : cols.stop // 16]),
-                mixed2[t][:, cols],
-                ADD,
-            )
-
-        last = PACK - 1
+        second_layer_tile(1)
+        centre = [centre_term(0)]
+        near, turned_z = [], []
         for t in range(PACK):
-            neighbours_1(t)
-        gate2_t = keep.tile([P, D, U], F32, name="gate2_t", tag="near0_0", align_bytes=64)
-        nc.scalar.activation(out=gate2_t[:], in_=gate2_raw[:], func=COPY, scale=0.8)
-        far = [keep.tile([P, D, U], F32, name="far", tag="far%d" % t, align_bytes=64) for t in range(PACK)]
-        for t in range(last):
-            for d in range(D):
-                gather_far(t, d, slice(0, U))
-            sum_far(t, slice(0, U), "turned_sb")
-        gather_far(last, 0, slice(0, U))
-        for cols, tag in zip(halves, ("turned_sb", "last_turned")):
-            for d in range(1, D):
-                gather_far(last, d, cols)
-            sum_far(last, cols, tag)
+            near.append(gated_terms(t, y[t], pos_t, gate_t, V, "near"))
+            if t == 0:
+                second_layer_tile(2)
+            if t + 1 < PACK:
+                centre.append(centre_term(t + 1))
+            turned_z.append(turn_and_add([centre[t]] + near[t], V, "turned_z%d" % t, "bank%d" % (3 + 2 * (t % 2))))
+            if t == 0:
+                second_layer_tile(3)
+            back = turn_back(turned_z[t], V, "bank%d" % (4 + 2 * (t % 2)))
+            nc.scalar.copy(out=z[t][:], in_=back[:])
 
-        result = keep.tile([P, PACK, U], F32, name="result", tag="far2", align_bytes=64)
-        for t in range(last):
-            restart_2(t, slice(0, U))
+        low, high = slice(0, U), slice(U, 2 * U)
+        roots = [near[1][2][:, low], near[1][2][:, high], near[2][2][:, low], near[2][2][:, high]]
+        thirds = {2: near[3][2][:, low], 3: turned_z[3][:, low]}
+        backs = {}
+        for t in range(PACK):
+            scalar_gather(roots[t], y[t], root_t, 0.25)
+            on_vector = nxt_t[:2] if t in thirds else nxt_t
+            terms = gated_terms(t, z[t], on_vector, gate2_raw, U, "far")
+            turned_out = turn_and_add([roots[t]] + terms, U, "turned_out%d" % t, "bank%d" % (4 + t % 2))
+            backs[t] = turn_back(turned_out, U, "bank%d" % ((7 + t) % 8))
+            if t in thirds:
+                scalar_gather(thirds[t], z[t], nxt_t[2], 0.8)
+            else:
+                nc.scalar.copy(out=result[:, t, :], in_=backs[t][:])
+                nc.sync.dma_start(out=out_rows[:, t, :], in_=result[:, t, :])
+        third_gated = keep.tile([P, 2, U], F32, name="third_gated", tag="far3_0", align_bytes=64)
+        for t in thirds:
+            nc.vector.tensor_tensor(third_gated[:, t - 2, :], thirds[t], gate2_raw[:, 2, :], MULT)
+        for t in thirds:
+            nc.vector.tensor_tensor(result[:, t, :], backs[t][:], third_gated[:, t - 2, :], ADD)
             nc.sync.dma_start(out=out_rows[:, t, :], in_=result[:, t, :])
-        for cols in halves:
-            restart_2(last, cols)
-        nc.sync.dma_start(out=out_rows[:, last, :], in_=result[:, last, :])
+        halves = [slice(0, U // 2), slice(U // 2, U)]
 
         out_codes = keep.tile([P, U], U32, align_bytes=64)
         out_sc = keep.tile([P, U], U8, align_bytes=64)
         result_bf = [
             keep.tile([P, U // 2, PACK], BF16, name="result_bf", tag=tag, align_bytes=64)
-            for tag in ("last_turned", "result_bf")
+            for tag in ("result_bf0", "result_bf1")
         ]
         for u, cols in enumerate(halves):
             dst = result_bf[u][:].rearrange("p (c i) t -> p c t i", i=4)

@@ -218,9 +218,9 @@ def tile_picked_zappnp_none_po_kernel(
                 stop=True,
             )
             if on_vector:
-                nc.vector.tensor_copy(out=y[t][:, cols], in_=bank[:])
+                nc.vector.tensor_scalar_mul(y[t][:, cols], bank[:], 0.2)
             else:
-                nc.scalar.copy(out=y[t][:, cols], in_=bank[:])
+                nc.scalar.activation(out=y[t][:, cols], in_=bank[:], func=COPY, scale=0.2)
 
         for chunk in range(S // CHUNK - 1):
             first = chunk * CHUNK
@@ -249,7 +249,7 @@ def tile_picked_zappnp_none_po_kernel(
             for u in range(2):
                 second_layer(t, slice(u * HALF, (u + 1) * HALF), False, "bank%d" % ((3 + 2 * t + u) % 8))
 
-        def turn_and_add(terms, width, name, tag):
+        def turn_and_add(terms, width, scale, name, tag):
             blocks = [slice(b * P, (b + 1) * P) for b in range(width // P)]
             turned = psum.tile([P, width], F32, name="turned", tag=tag)
             for i, term in enumerate(terms):
@@ -261,7 +261,7 @@ def tile_picked_zappnp_none_po_kernel(
                         is_transpose=True,
                     )
             turned_sb = keep.tile([P, width], F32, name=name, align_bytes=64)
-            nc.scalar.activation(out=turned_sb[:], in_=turned[:], func=COPY, scale=0.8)
+            nc.scalar.activation(out=turned_sb[:], in_=turned[:], func=COPY, scale=scale)
             return turned_sb
 
         def turn_back(turned_sb, width, tag):
@@ -300,34 +300,37 @@ def tile_picked_zappnp_none_po_kernel(
                 second_layer_tile(2)
             if t + 1 < PACK:
                 centre.append(centre_term(t + 1))
-            turned_z.append(turn_and_add([centre[t]] + near[t], V, "turned_z%d" % t, "bank%d" % (3 + 2 * (t % 2))))
+            turned_z.append(turn_and_add([centre[t]] + near[t], V, 4.0, "turned_z%d" % t, "bank%d" % (3 + 2 * (t % 2))))
             if t == 0:
                 second_layer_tile(3)
             back = turn_back(turned_z[t], V, "bank%d" % (4 + 2 * (t % 2)))
             nc.scalar.copy(out=z[t][:], in_=back[:])
 
         low, high = slice(0, U), slice(U, 2 * U)
-        roots = [near[1][2][:, low], near[1][2][:, high], near[2][2][:, low], near[2][2][:, high]]
-        thirds = {2: near[3][2][:, low], 3: turned_z[3][:, low]}
-        backs = {}
-        for t in range(PACK):
-            scalar_gather(roots[t], y[t], root_t, 0.25)
-            on_vector = nxt_t[:2] if t in thirds else nxt_t
-            terms = gated_terms(t, z[t], on_vector, gate2_raw, U, "far")
-            turned_out = turn_and_add([roots[t]] + terms, U, "turned_out%d" % t, "bank%d" % (4 + t % 2))
-            backs[t] = turn_back(turned_out, U, "bank%d" % ((7 + t) % 8))
-            if t in thirds:
-                scalar_gather(thirds[t], z[t], nxt_t[2], 0.8)
-            else:
-                nc.scalar.copy(out=result[:, t, :], in_=backs[t][:])
-                nc.sync.dma_start(out=out_rows[:, t, :], in_=result[:, t, :])
-        third_gated = keep.tile([P, 2, U], F32, name="third_gated", tag="far3_0", align_bytes=64)
-        for t in thirds:
-            nc.vector.tensor_tensor(third_gated[:, t - 2, :], thirds[t], gate2_raw[:, 2, :], MULT)
-        for t in thirds:
-            nc.vector.tensor_tensor(result[:, t, :], backs[t][:], third_gated[:, t - 2, :], ADD)
-            nc.sync.dma_start(out=out_rows[:, t, :], in_=result[:, t, :])
         halves = [slice(0, U // 2), slice(U // 2, U)]
+        roots = {1: near[1][2][:, low], 2: near[1][2][:, high], 3: near[3][2][:, low]}
+        plain = [near[2][2][:, low], near[2][2][:, high], turned_z[3][:, low]]
+        for d in range(D):
+            scalar_gather(plain[d], z[0], nxt_t[d], 0.8)
+        for t in range(1, PACK):
+            scalar_gather(roots[t], y[t], root_t, 1.25)
+            terms = gated_terms(t, z[t], nxt_t, gate2_raw, U, "far")
+            turned_out = turn_and_add([roots[t]] + terms, U, 0.8, "turned_out%d" % t, "bank%d" % (5 - t % 2))
+            back = turn_back(turned_out, U, "bank%d" % ((6 + t) % 8))
+            nc.scalar.copy(out=result[:, t, :], in_=back[:])
+            nc.sync.dma_start(out=out_rows[:, t, :], in_=result[:, t, :])
+
+        first_two = gate2_raw[:, :2, :].rearrange("p d x -> p (d x)")
+        nc.vector.tensor_tensor(first_two, near[2][2][:], first_two, MULT)
+        nc.vector.tensor_tensor(gate2_raw[:, 2, :], plain[2], gate2_raw[:, 2, :], MULT)
+        pair_sums = keep.tile([P, 2, U], F32, align_bytes=64)
+        nc.vector.tensor_tensor(pair_sums[:, 0, :], gate2_raw[:, 0, :], gate2_raw[:, 1, :], ADD)
+        for cols in halves:
+            offsets = root_t[:, cols.start // 16 : cols.stop // 16]
+            nc.vector.tensor_tensor(pair_sums[:, 1, cols], y[0][:].indirect(offsets), gate2_raw[:, 2, cols], ADD)
+        for cols in halves:
+            nc.vector.tensor_tensor(result[:, 0, cols], pair_sums[:, 0, cols], pair_sums[:, 1, cols], ADD)
+        nc.sync.dma_start(out=out_rows[:, 0, :], in_=result[:, 0, :])
 
         out_codes = keep.tile([P, U], U32, align_bytes=64)
         out_sc = keep.tile([P, U], U8, align_bytes=64)

@@ -308,29 +308,40 @@ def tile_picked_zappnp_none_po_kernel(
 
         low, high = slice(0, U), slice(U, 2 * U)
         halves = [slice(0, U // 2), slice(U // 2, U)]
-        roots = {1: near[1][2][:, low], 2: near[1][2][:, high], 3: near[3][2][:, low]}
-        plain = [near[2][2][:, low], near[2][2][:, high], turned_z[3][:, low]]
-        for d in range(D):
-            scalar_gather(plain[d], z[0], nxt_t[d], 0.8)
+        last = PACK - 1
+        third_last = keep.tile([P, U], F32, align_bytes=64)
+        scalar_gather(third_last[:], z[last], nxt_t[2], 0.8)
+        roots = {1: near[1][2][:, low], 2: near[1][2][:, high], 3: turned_z[2][:, low]}
+        for d, cols in ((1, low), (2, high)):
+            scalar_gather(near[2][2][:, cols], z[0], nxt_t[d], 0.8)
         for t in range(1, PACK):
             scalar_gather(roots[t], y[t], root_t, 1.25)
-            terms = gated_terms(t, z[t], nxt_t, gate2_raw, U, "far")
+            terms = gated_terms(t, z[t], nxt_t if t < last else nxt_t[:2], gate2_raw, U, "far")
             turned_out = turn_and_add([roots[t]] + terms, U, 0.8, "turned_out%d" % t, "bank%d" % (5 - t % 2))
+            if t == 1:
+                plain_first = terms[0]
+                scalar_gather(plain_first[:], z[0], nxt_t[0], 0.8)
             back = turn_back(turned_out, U, "bank%d" % ((6 + t) % 8))
-            nc.scalar.copy(out=result[:, t, :], in_=back[:])
-            nc.sync.dma_start(out=out_rows[:, t, :], in_=result[:, t, :])
+            if t < last:
+                nc.scalar.copy(out=result[:, t, :], in_=back[:])
+                nc.sync.dma_start(out=out_rows[:, t, :], in_=result[:, t, :])
 
-        first_two = gate2_raw[:, :2, :].rearrange("p d x -> p (d x)")
-        nc.vector.tensor_tensor(first_two, near[2][2][:], first_two, MULT)
-        nc.vector.tensor_tensor(gate2_raw[:, 2, :], plain[2], gate2_raw[:, 2, :], MULT)
+        nc.vector.tensor_tensor(near[2][2][:, high], near[2][2][:, high], gate2_raw[:, 2, :], MULT)
+        nc.vector.tensor_tensor(third_last[:], third_last[:], gate2_raw[:, 2, :], MULT)
+        nc.vector.tensor_tensor(gate2_raw[:, 0, :], plain_first[:], gate2_raw[:, 0, :], MULT)
+        nc.vector.tensor_tensor(gate2_raw[:, 1, :], near[2][2][:, low], gate2_raw[:, 1, :], MULT)
         pair_sums = keep.tile([P, 2, U], F32, align_bytes=64)
-        nc.vector.tensor_tensor(pair_sums[:, 0, :], gate2_raw[:, 0, :], gate2_raw[:, 1, :], ADD)
-        for cols in halves:
+        for u, cols in enumerate(halves):
             offsets = root_t[:, cols.start // 16 : cols.stop // 16]
-            nc.vector.tensor_tensor(pair_sums[:, 1, cols], y[0][:].indirect(offsets), gate2_raw[:, 2, cols], ADD)
+            nc.vector.tensor_tensor(pair_sums[:, 0, cols], y[0][:].indirect(offsets), gate2_raw[:, 0, cols], ADD)
+            if u == 0:
+                nc.vector.tensor_tensor(pair_sums[:, 1, :], gate2_raw[:, 1, :], near[2][2][:, high], ADD)
         for cols in halves:
             nc.vector.tensor_tensor(result[:, 0, cols], pair_sums[:, 0, cols], pair_sums[:, 1, cols], ADD)
         nc.sync.dma_start(out=out_rows[:, 0, :], in_=result[:, 0, :])
+        for cols in halves:
+            nc.vector.tensor_tensor(result[:, last, cols], back[:, cols], third_last[:, cols], ADD)
+        nc.sync.dma_start(out=out_rows[:, last, :], in_=result[:, last, :])
 
         out_codes = keep.tile([P, U], U32, align_bytes=64)
         out_sc = keep.tile([P, U], U8, align_bytes=64)

@@ -25,7 +25,7 @@ PIECES = ((0, 512), (512, 768), (768, 896), (896, 1024))
 PIECE_ORDER = (0, 1, 2, 3)
 VECTOR_CHUNKS = (2, 4)
 Y_PIECES = PIECES
-WARM = 3
+WARM = 2
 SCALAR_ROWS = 48
 LAST_SCALAR_ROWS = 32
 FIRST_WORDS = 1280
@@ -154,9 +154,9 @@ def tile_picked_zappnp_none_po_kernel(
             nc.tensor.matmul_mx(
                 out=warm[:],
                 lhsT=x_codes[0][:, t * P : (t + 1) * P].bitcast(FP8X4),
-                lhsT_scale=x_sc_spread[:, t * P : (t + 1) * P],
+                lhsT_scale=w2_sc[t],
                 rhs=x_codes[0][:].bitcast(FP8X4),
-                rhs_scale=x_sc_spread[:, :HALF],
+                rhs_scale=w2_sc_dealt[:].rearrange("p t m -> p (t m)"),
                 start=True,
                 stop=True,
             )
@@ -247,7 +247,7 @@ def tile_picked_zappnp_none_po_kernel(
 
         def second_layer_tile(t):
             for u in range(2):
-                second_layer(t, slice(u * HALF, (u + 1) * HALF), False, "bank%d" % ((3 + 2 * t + u) % 8))
+                second_layer(t, slice(u * HALF, (u + 1) * HALF), False, (("bank5", "bank6"), ("bank7", "bank0"), ("bank7", "bank0"))[t - 1][u])
 
         def turn_and_add(terms, width, scale, name, tag):
             blocks = [slice(b * P, (b + 1) * P) for b in range(width // P)]
@@ -296,10 +296,10 @@ def tile_picked_zappnp_none_po_kernel(
         near, turned_z = [], []
         for t in range(PACK):
             near.append(gated_terms(t, y[t], pos_t, gate_t, V, "near"))
-            if t == 0:
-                second_layer_tile(2)
             if t + 1 < PACK:
                 centre.append(centre_term(t + 1))
+            if t == 0:
+                second_layer_tile(2)
             turned_z.append(turn_and_add([centre[t]] + near[t], V, 4.0, "turned_z%d" % t, "bank%d" % (3 + 2 * (t % 2))))
             if t == 0:
                 second_layer_tile(3)
@@ -321,6 +321,9 @@ def tile_picked_zappnp_none_po_kernel(
             if t == 1:
                 plain_first = terms[0]
                 scalar_gather(plain_first[:], z[0], nxt_t[0], 0.8)
+            if t == 2:
+                root_first = terms[0]
+                scalar_gather(root_first[:], y[0], root_t, 1.0)
             back = turn_back(turned_out, U, "bank%d" % ((6 + t) % 8))
             if t < last:
                 nc.scalar.copy(out=result[:, t, :], in_=back[:])
@@ -329,15 +332,13 @@ def tile_picked_zappnp_none_po_kernel(
         nc.vector.tensor_tensor(near[2][2][:, high], near[2][2][:, high], gate2_raw[:, 2, :], MULT)
         nc.vector.tensor_tensor(third_last[:], third_last[:], gate2_raw[:, 2, :], MULT)
         nc.vector.tensor_tensor(gate2_raw[:, 0, :], plain_first[:], gate2_raw[:, 0, :], MULT)
+        partial = keep.tile([P, 2, U], F32, align_bytes=64)
+        nc.vector.tensor_tensor(partial[:, 0, :], near[2][2][:, high], root_first[:], ADD)
         nc.vector.tensor_tensor(gate2_raw[:, 1, :], near[2][2][:, low], gate2_raw[:, 1, :], MULT)
-        pair_sums = keep.tile([P, 2, U], F32, align_bytes=64)
-        for u, cols in enumerate(halves):
-            offsets = root_t[:, cols.start // 16 : cols.stop // 16]
-            nc.vector.tensor_tensor(pair_sums[:, 0, cols], y[0][:].indirect(offsets), gate2_raw[:, 0, cols], ADD)
-            if u == 0:
-                nc.vector.tensor_tensor(pair_sums[:, 1, :], gate2_raw[:, 1, :], near[2][2][:, high], ADD)
         for cols in halves:
-            nc.vector.tensor_tensor(result[:, 0, cols], pair_sums[:, 0, cols], pair_sums[:, 1, cols], ADD)
+            nc.vector.tensor_tensor(partial[:, 1, cols], partial[:, 0, cols], gate2_raw[:, 0, cols], ADD)
+        for cols in halves:
+            nc.vector.tensor_tensor(result[:, 0, cols], partial[:, 1, cols], gate2_raw[:, 1, cols], ADD)
         nc.sync.dma_start(out=out_rows[:, 0, :], in_=result[:, 0, :])
         for cols in halves:
             nc.vector.tensor_tensor(result[:, last, cols], back[:, cols], third_last[:, cols], ADD)

@@ -314,34 +314,41 @@ def tile_picked_zappnp_none_po_kernel(
         roots = {1: near[1][2][:, low], 2: near[1][2][:, high], 3: turned_z[2][:, low]}
         for d, cols in ((1, low), (2, high)):
             scalar_gather(near[2][2][:, cols], z[0], nxt_t[d], 0.8)
-        for t in range(1, PACK):
+        for t in range(1, last):
             scalar_gather(roots[t], y[t], root_t, 1.25)
-            terms = gated_terms(t, z[t], nxt_t if t < last else nxt_t[:2], gate2_raw, U, "far")
+            terms = gated_terms(t, z[t], nxt_t, gate2_raw, U, "far")
             turned_out = turn_and_add([roots[t]] + terms, U, 0.8, "turned_out%d" % t, "bank%d" % (5 - t % 2))
             if t == 1:
                 plain_first = terms[0]
                 scalar_gather(plain_first[:], z[0], nxt_t[0], 0.8)
-            if t == 2:
-                root_first = terms[0]
-                scalar_gather(root_first[:], y[0], root_t, 1.0)
             back = turn_back(turned_out, U, "bank%d" % ((6 + t) % 8))
-            if t < last:
-                nc.scalar.copy(out=result[:, t, :], in_=back[:])
-                nc.sync.dma_start(out=out_rows[:, t, :], in_=result[:, t, :])
+            nc.scalar.copy(out=result[:, t, :], in_=back[:])
+            nc.sync.dma_start(out=out_rows[:, t, :], in_=result[:, t, :])
+        scalar_gather(roots[last], y[last], root_t, 1.25)
+        first_term = gated_terms(last, z[last], nxt_t[:1], gate2_raw, U, "far")[0]
+        second_term = keep.tile([P, U], F32, align_bytes=64)
+        backs = []
+        for u, cols in enumerate(halves):
+            offsets = nxt_t[1][:, cols.start // 16 : cols.stop // 16]
+            nc.vector.tensor_tensor(second_term[:, cols], z[last][:].indirect(offsets), gate2_raw[:, 1, cols], MULT)
+            terms = [roots[last][:, cols], first_term[:, cols], second_term[:, cols]]
+            turned_half = turn_and_add(terms, U // 2, 0.8, "turned_half%d" % u, ("bank4", "bank3")[u])
+            backs.append(turn_back(turned_half, U // 2, ("bank1", "bank2")[u]))
 
-        nc.vector.tensor_tensor(near[2][2][:, high], near[2][2][:, high], gate2_raw[:, 2, :], MULT)
+        nc.vector.tensor_tensor(near[2][2][:], near[2][2][:], gate2_raw[:, 1:, :].rearrange("p d x -> p (d x)"), MULT)
         nc.vector.tensor_tensor(third_last[:], third_last[:], gate2_raw[:, 2, :], MULT)
         nc.vector.tensor_tensor(gate2_raw[:, 0, :], plain_first[:], gate2_raw[:, 0, :], MULT)
-        partial = keep.tile([P, 2, U], F32, align_bytes=64)
-        nc.vector.tensor_tensor(partial[:, 0, :], near[2][2][:, high], root_first[:], ADD)
-        nc.vector.tensor_tensor(gate2_raw[:, 1, :], near[2][2][:, low], gate2_raw[:, 1, :], MULT)
+        with_root = keep.tile([P, U], F32, align_bytes=64)
+        for u, cols in enumerate(halves):
+            offsets = root_t[:, cols.start // 16 : cols.stop // 16]
+            nc.vector.tensor_tensor(with_root[:, cols], y[0][:].indirect(offsets), gate2_raw[:, 0, cols], ADD)
+            if u == 0:
+                nc.vector.tensor_tensor(gate2_raw[:, 1, :], near[2][2][:, low], near[2][2][:, high], ADD)
         for cols in halves:
-            nc.vector.tensor_tensor(partial[:, 1, cols], partial[:, 0, cols], gate2_raw[:, 0, cols], ADD)
-        for cols in halves:
-            nc.vector.tensor_tensor(result[:, 0, cols], partial[:, 1, cols], gate2_raw[:, 1, cols], ADD)
+            nc.vector.tensor_tensor(result[:, 0, cols], with_root[:, cols], gate2_raw[:, 1, cols], ADD)
         nc.sync.dma_start(out=out_rows[:, 0, :], in_=result[:, 0, :])
-        for cols in halves:
-            nc.vector.tensor_tensor(result[:, last, cols], back[:, cols], third_last[:, cols], ADD)
+        for back, cols in zip(backs, halves):
+            nc.vector.tensor_tensor(result[:, last, cols], back[:], third_last[:, cols], ADD)
         nc.sync.dma_start(out=out_rows[:, last, :], in_=result[:, last, :])
 
         out_codes = keep.tile([P, U], U32, align_bytes=64)

@@ -321,6 +321,9 @@ def tile_picked_zappnp_none_po_kernel(
             if t == 1:
                 plain_first = terms[0]
                 scalar_gather(plain_first[:], z[0], nxt_t[0], 0.8)
+            else:
+                root_first = terms[0]
+                scalar_gather(root_first[:], y[0], root_t, 1.0)
             back = turn_back(turned_out, U, "bank%d" % ((6 + t) % 8))
             nc.scalar.copy(out=result[:, t, :], in_=back[:])
             nc.sync.dma_start(out=out_rows[:, t, :], in_=result[:, t, :])
@@ -338,12 +341,10 @@ def tile_picked_zappnp_none_po_kernel(
         nc.vector.tensor_tensor(near[2][2][:], near[2][2][:], gate2_raw[:, 1:, :].rearrange("p d x -> p (d x)"), MULT)
         nc.vector.tensor_tensor(third_last[:], third_last[:], gate2_raw[:, 2, :], MULT)
         nc.vector.tensor_tensor(gate2_raw[:, 0, :], plain_first[:], gate2_raw[:, 0, :], MULT)
+        nc.vector.tensor_tensor(gate2_raw[:, 1, :], near[2][2][:, low], near[2][2][:, high], ADD)
         with_root = keep.tile([P, U], F32, align_bytes=64)
-        for u, cols in enumerate(halves):
-            offsets = root_t[:, cols.start // 16 : cols.stop // 16]
-            nc.vector.tensor_tensor(with_root[:, cols], y[0][:].indirect(offsets), gate2_raw[:, 0, cols], ADD)
-            if u == 0:
-                nc.vector.tensor_tensor(gate2_raw[:, 1, :], near[2][2][:, low], near[2][2][:, high], ADD)
+        for cols in halves:
+            nc.vector.tensor_tensor(with_root[:, cols], root_first[:, cols], gate2_raw[:, 0, cols], ADD)
         for cols in halves:
             nc.vector.tensor_tensor(result[:, 0, cols], with_root[:, cols], gate2_raw[:, 1, cols], ADD)
         nc.sync.dma_start(out=out_rows[:, 0, :], in_=result[:, 0, :])

@@ -314,19 +314,22 @@ def tile_picked_zappnp_none_po_kernel(
         roots = {1: near[1][2][:, low], 2: near[1][2][:, high], 3: turned_z[2][:, low]}
         for d, cols in ((1, low), (2, high)):
             scalar_gather(near[2][2][:, cols], z[0], nxt_t[d], 0.8)
-        for t in range(1, last):
-            scalar_gather(roots[t], y[t], root_t, 1.25)
-            terms = gated_terms(t, z[t], nxt_t, gate2_raw, U, "far")
-            turned_out = turn_and_add([roots[t]] + terms, U, 0.8, "turned_out%d" % t, "bank%d" % (5 - t % 2))
-            if t == 1:
-                plain_first = terms[0]
-                scalar_gather(plain_first[:], z[0], nxt_t[0], 0.8)
-            else:
-                root_first = terms[0]
-                scalar_gather(root_first[:], y[0], root_t, 1.0)
-            back = turn_back(turned_out, U, "bank%d" % ((6 + t) % 8))
-            nc.scalar.copy(out=result[:, t, :], in_=back[:])
-            nc.sync.dma_start(out=out_rows[:, t, :], in_=result[:, t, :])
+        scalar_gather(roots[1], y[1], root_t, 1.25)
+        terms = gated_terms(1, z[1], nxt_t, gate2_raw, U, "far")
+        turned_out = turn_and_add([roots[1]] + terms, U, 0.8, "turned_out1", "bank4")
+        plain_first = terms[0]
+        scalar_gather(plain_first[:], z[0], nxt_t[0], 0.8)
+        back = turn_back(turned_out, U, "bank7")
+        nc.scalar.copy(out=result[:, 1, :], in_=back[:])
+        nc.sync.dma_start(out=out_rows[:, 1, :], in_=result[:, 1, :])
+
+        scalar_gather(roots[2], y[2], root_t, 1.0)
+        terms = gated_terms(2, z[2], nxt_t, gate2_raw, U, "far")
+        turned_out = turn_and_add(terms, U, 0.8, "turned_out2", "bank5")
+        root_first = terms[0]
+        scalar_gather(root_first[:], y[0], root_t, 1.0)
+        back_two = turn_back(turned_out, U, "bank0")
+
         scalar_gather(roots[last], y[last], root_t, 1.25)
         first_term = gated_terms(last, z[last], nxt_t[:1], gate2_raw, U, "far")[0]
         second_term = keep.tile([P, U], F32, align_bytes=64)
@@ -342,6 +345,8 @@ def tile_picked_zappnp_none_po_kernel(
         nc.vector.tensor_tensor(third_last[:], third_last[:], gate2_raw[:, 2, :], MULT)
         nc.vector.tensor_tensor(gate2_raw[:, 0, :], plain_first[:], gate2_raw[:, 0, :], MULT)
         nc.vector.tensor_tensor(gate2_raw[:, 1, :], near[2][2][:, low], near[2][2][:, high], ADD)
+        nc.vector.tensor_tensor(result[:, 2, :], back_two[:], roots[2], ADD)
+        nc.sync.dma_start(out=out_rows[:, 2, :], in_=result[:, 2, :])
         with_root = keep.tile([P, U], F32, align_bytes=64)
         for cols in halves:
             nc.vector.tensor_tensor(with_root[:, cols], root_first[:, cols], gate2_raw[:, 0, cols], ADD)

@@ -345,14 +345,14 @@ def tile_picked_zappnp_none_po_kernel(
         nc.vector.tensor_tensor(third_last[:], third_last[:], gate2_raw[:, 2, :], MULT)
         nc.vector.tensor_tensor(gate2_raw[:, 0, :], plain_first[:], gate2_raw[:, 0, :], MULT)
         nc.vector.tensor_tensor(gate2_raw[:, 1, :], near[2][2][:, low], near[2][2][:, high], ADD)
-        nc.vector.tensor_tensor(result[:, 2, :], back_two[:], roots[2], ADD)
-        nc.sync.dma_start(out=out_rows[:, 2, :], in_=result[:, 2, :])
         with_root = keep.tile([P, U], F32, align_bytes=64)
         for cols in halves:
             nc.vector.tensor_tensor(with_root[:, cols], root_first[:, cols], gate2_raw[:, 0, cols], ADD)
         for cols in halves:
             nc.vector.tensor_tensor(result[:, 0, cols], with_root[:, cols], gate2_raw[:, 1, cols], ADD)
         nc.sync.dma_start(out=out_rows[:, 0, :], in_=result[:, 0, :])
+        nc.vector.tensor_tensor(result[:, 2, :], back_two[:], roots[2], ADD)
+        nc.sync.dma_start(out=out_rows[:, 2, :], in_=result[:, 2, :])
         for back, cols in zip(backs, halves):
             nc.vector.tensor_tensor(result[:, last, cols], back[:], third_last[:, cols], ADD)
         nc.sync.dma_start(out=out_rows[:, last, :], in_=result[:, last, :])

@@ -273,7 +273,6 @@ def tile_picked_zappnp_none_po_kernel(
 
         z = [keep.tile([P, V], F32, name="z", tag="z%d" % t, align_bytes=64) for t in range(PACK)]
         out_rows = out_0.rearrange("(p t) x -> p t x", t=PACK)
-        result = keep.tile([P, PACK, U], F32, name="result", align_bytes=64)
 
         def gated_terms(t, window, near_lists, gates, width, tag):
             terms = []
@@ -314,18 +313,16 @@ def tile_picked_zappnp_none_po_kernel(
         roots = {1: near[1][2][:, low], 2: near[1][2][:, high], 3: turned_z[2][:, low]}
         for d, cols in ((1, low), (2, high)):
             scalar_gather(near[2][2][:, cols], z[0], nxt_t[d], 0.8)
-        scalar_gather(roots[1], y[1], root_t, 1.25)
+        scalar_gather(roots[1], y[1], root_t, 1.0)
         terms = gated_terms(1, z[1], nxt_t, gate2_raw, U, "far")
-        turned_out = turn_and_add([roots[1]] + terms, U, 0.8, "turned_out1", "bank4")
-        plain_first = terms[0]
+        turned_out = turn_and_add(terms, U, 0.8, "turned_out1", "bank4")
+        plain_first = terms[1]
         scalar_gather(plain_first[:], z[0], nxt_t[0], 0.8)
-        back = turn_back(turned_out, U, "bank7")
-        nc.scalar.copy(out=result[:, 1, :], in_=back[:])
-        nc.sync.dma_start(out=out_rows[:, 1, :], in_=result[:, 1, :])
+        back_one = turn_back(turned_out, U, "bank7")
 
-        scalar_gather(roots[2], y[2], root_t, 1.0)
+        scalar_gather(roots[2], y[2], root_t, 1.25)
         terms = gated_terms(2, z[2], nxt_t, gate2_raw, U, "far")
-        turned_out = turn_and_add(terms, U, 0.8, "turned_out2", "bank5")
+        turned_out = turn_and_add([roots[2]] + terms, U, 0.8, "turned_out2", "bank5")
         root_first = terms[0]
         scalar_gather(root_first[:], y[0], root_t, 1.0)
         back_two = turn_back(turned_out, U, "bank0")
@@ -341,18 +338,22 @@ def tile_picked_zappnp_none_po_kernel(
             turned_half = turn_and_add(terms, U // 2, 0.8, "turned_half%d" % u, ("bank4", "bank3")[u])
             backs.append(turn_back(turned_half, U // 2, ("bank1", "bank2")[u]))
 
+        result = keep.tile([P, PACK, U], F32, name="result", tag="far3_0", align_bytes=64)
+        nc.scalar.copy(out=result[:, 2, :], in_=back_two[:])
+        nc.sync.dma_start(out=out_rows[:, 2, :], in_=result[:, 2, :])
+
         nc.vector.tensor_tensor(near[2][2][:], near[2][2][:], gate2_raw[:, 1:, :].rearrange("p d x -> p (d x)"), MULT)
         nc.vector.tensor_tensor(third_last[:], third_last[:], gate2_raw[:, 2, :], MULT)
         nc.vector.tensor_tensor(gate2_raw[:, 0, :], plain_first[:], gate2_raw[:, 0, :], MULT)
         nc.vector.tensor_tensor(gate2_raw[:, 1, :], near[2][2][:, low], near[2][2][:, high], ADD)
+        nc.vector.tensor_tensor(result[:, 1, :], back_one[:], roots[1], ADD)
+        nc.sync.dma_start(out=out_rows[:, 1, :], in_=result[:, 1, :])
         with_root = keep.tile([P, U], F32, align_bytes=64)
         for cols in halves:
             nc.vector.tensor_tensor(with_root[:, cols], root_first[:, cols], gate2_raw[:, 0, cols], ADD)
         for cols in halves:
             nc.vector.tensor_tensor(result[:, 0, cols], with_root[:, cols], gate2_raw[:, 1, cols], ADD)
         nc.sync.dma_start(out=out_rows[:, 0, :], in_=result[:, 0, :])
-        nc.vector.tensor_tensor(result[:, 2, :], back_two[:], roots[2], ADD)
-        nc.sync.dma_start(out=out_rows[:, 2, :], in_=result[:, 2, :])
         for back, cols in zip(backs, halves):
             nc.vector.tensor_tensor(result[:, last, cols], back[:], third_last[:, cols], ADD)
         nc.sync.dma_start(out=out_rows[:, last, :], in_=result[:, last, :])

@@ -29,6 +29,7 @@ WARM = 2
 SCALAR_ROWS = 48
 LAST_SCALAR_ROWS = 32
 FIRST_WORDS = 1280
+PLAIN_TERMS = (2, 1, 1)
 
 
 def tile_picked_zappnp_none_po_kernel(
@@ -39,7 +40,6 @@ def tile_picked_zappnp_none_po_kernel(
     with ExitStack() as ctx:
         lists = ctx.enter_context(tc.tile_pool(name="lists", bufs=1))
         keep = ctx.enter_context(tc.tile_pool(name="keep", bufs=1))
-        ring = ctx.enter_context(tc.tile_pool(name="ring", bufs=2))
         psum = ctx.enter_context(tc.psum_pool(name="psum", bufs=1))
 
         def load_list(name, source):
@@ -245,9 +245,9 @@ def tile_picked_zappnp_none_po_kernel(
         nc.vector.tensor_copy(out=w2_codes_rest[:].rearrange("p t m -> p m t"), in_=w2_word_view[:, :, 1:])
         w2_codes.extend(w2_codes_rest[:, t, :] for t in range(PACK - 1))
 
-        def second_layer_tile(t):
+        def second_layer_tile(t, banks):
             for u in range(2):
-                second_layer(t, slice(u * HALF, (u + 1) * HALF), False, (("bank5", "bank6"), ("bank7", "bank0"), ("bank7", "bank0"))[t - 1][u])
+                second_layer(t, slice(u * HALF, (u + 1) * HALF), False, banks[u])
 
         def turn_and_add(terms, width, scale, name, tag):
             blocks = [slice(b * P, (b + 1) * P) for b in range(width // P)]
@@ -260,104 +260,132 @@ def tile_picked_zappnp_none_po_kernel(
                         stop=(i == len(terms) - 1 and b == len(blocks) - 1),
                         is_transpose=True,
                     )
-            turned_sb = keep.tile([P, width], F32, name=name, align_bytes=64)
+            turned_sb = keep.tile([P, width], F32, name="turned_sb", tag=name, align_bytes=64)
             nc.scalar.activation(out=turned_sb[:], in_=turned[:], func=COPY, scale=scale)
             return turned_sb
 
-        def turn_back(turned_sb, width, tag):
+        def turn_back(turned_sb, width, tag, dst):
             back = psum.tile([P, width], F32, name="back", tag=tag)
             for b in range(width // P):
                 cols = slice(b * P, (b + 1) * P)
                 nc.tensor.transpose(back[:, cols], turned_sb[:, cols], identity[:])
-            return back
+            nc.scalar.copy(out=dst, in_=back[:])
 
-        z = [keep.tile([P, V], F32, name="z", tag="z%d" % t, align_bytes=64) for t in range(PACK)]
-        out_rows = out_0.rearrange("(p t) x -> p t x", t=PACK)
+        def gated_gather(dst, window, offsets, gates):
+            nc.vector.tensor_tensor(dst, window[:].indirect(offsets), gates, MULT)
 
-        def gated_terms(t, window, near_lists, gates, width, tag):
-            terms = []
-            for d, near in enumerate(near_lists):
-                term = keep.tile([P, width], F32, name="near", tag="%s%d_%d" % (tag, t, d), align_bytes=64)
-                nc.vector.tensor_tensor(term[:], window[:].indirect(near[:]), gates[:, d, :], MULT)
-                terms.append(term)
-            return terms
-
-        def scalar_gather(dst, window, offsets, scale):
-            nc.scalar.activation(out=dst, in_=window[:].indirect(offsets[:]), func=COPY, scale=scale)
+        def plain_gather(dst, window, offsets):
+            nc.scalar.activation(out=dst, in_=window[:].indirect(offsets), func=COPY)
 
         def centre_term(t):
-            own = ring.tile([P, V], F32, name="own", tag="own", align_bytes=64)
-            scalar_gather(own[:], y[t], cen_t, 0.25)
-            return own
+            own = keep.tile([P, V], F32, name="own%d" % t, align_bytes=64)
+            nc.scalar.activation(out=own[:], in_=y[t][:].indirect(cen_t[:]), func=COPY, scale=0.25)
+            return own[:]
 
-        second_layer_tile(1)
-        centre = [centre_term(0)]
-        near, turned_z = [], []
-        for t in range(PACK):
-            near.append(gated_terms(t, y[t], pos_t, gate_t, V, "near"))
-            if t + 1 < PACK:
-                centre.append(centre_term(t + 1))
-            if t == 0:
-                second_layer_tile(2)
-            turned_z.append(turn_and_add([centre[t]] + near[t], V, 4.0, "turned_z%d" % t, "bank%d" % (3 + 2 * (t % 2))))
-            if t == 0:
-                second_layer_tile(3)
-            back = turn_back(turned_z[t], V, "bank%d" % (4 + 2 * (t % 2)))
-            nc.scalar.copy(out=z[t][:], in_=back[:])
+        def near_terms(t):
+            terms = []
+            for d in range(D):
+                term = keep.tile([P, V], F32, name="near", tag="near%d_%d" % (t, d), align_bytes=64)
+                gated_gather(term[:], y[t], pos_t[d][:], gate_t[:, d, :])
+                terms.append(term[:])
+            return terms
 
-        low, high = slice(0, U), slice(U, 2 * U)
-        halves = [slice(0, U // 2), slice(U // 2, U)]
         last = PACK - 1
-        third_last = keep.tile([P, U], F32, align_bytes=64)
-        scalar_gather(third_last[:], z[last], nxt_t[2], 0.8)
-        roots = {1: near[1][2][:, low], 2: near[1][2][:, high], 3: turned_z[2][:, low]}
-        for d, cols in ((1, low), (2, high)):
-            scalar_gather(near[2][2][:, cols], z[0], nxt_t[d], 0.8)
-        scalar_gather(roots[1], y[1], root_t, 1.0)
-        terms = gated_terms(1, z[1], nxt_t, gate2_raw, U, "far")
-        turned_out = turn_and_add(terms, U, 0.8, "turned_out1", "bank4")
-        plain_first = terms[1]
-        scalar_gather(plain_first[:], z[0], nxt_t[0], 0.8)
-        back_one = turn_back(turned_out, U, "bank7")
+        z = [keep.tile([P, V], F32, name="z%d" % t, align_bytes=64) for t in range(PACK)]
+        roots = []
+        plain = [keep.tile([P, n * U], F32, name="plain%d" % t, align_bytes=64) for t, n in enumerate(PLAIN_TERMS) if n]
+        out_rows = out_0.rearrange("(p t) x -> p t x", t=PACK)
 
-        scalar_gather(roots[2], y[2], root_t, 1.25)
-        terms = gated_terms(2, z[2], nxt_t, gate2_raw, U, "far")
-        turned_out = turn_and_add([roots[2]] + terms, U, 0.8, "turned_out2", "bank5")
-        root_first = terms[0]
-        scalar_gather(root_first[:], y[0], root_t, 1.0)
-        back_two = turn_back(turned_out, U, "bank0")
+        def plain_term(t, d):
+            plain_gather(plain[t][:, d * U : (d + 1) * U], z[t], nxt_t[d][:])
 
-        scalar_gather(roots[last], y[last], root_t, 1.25)
-        first_term = gated_terms(last, z[last], nxt_t[:1], gate2_raw, U, "far")[0]
-        second_term = keep.tile([P, U], F32, align_bytes=64)
-        backs = []
-        for u, cols in enumerate(halves):
-            offsets = nxt_t[1][:, cols.start // 16 : cols.stop // 16]
-            nc.vector.tensor_tensor(second_term[:, cols], z[last][:].indirect(offsets), gate2_raw[:, 1, cols], MULT)
-            terms = [roots[last][:, cols], first_term[:, cols], second_term[:, cols]]
-            turned_half = turn_and_add(terms, U // 2, 0.8, "turned_half%d" % u, ("bank4", "bank3")[u])
-            backs.append(turn_back(turned_half, U // 2, ("bank1", "bank2")[u]))
+        def root_term(t, tag):
+            roots.append(keep.tile([P, U], F32, name="root", tag=tag, align_bytes=64))
+            plain_gather(roots[t][:], y[t], root_t[:])
 
-        result = keep.tile([P, PACK, U], F32, name="result", tag="far3_0", align_bytes=64)
-        nc.scalar.copy(out=result[:, 2, :], in_=back_two[:])
-        nc.sync.dma_start(out=out_rows[:, 2, :], in_=result[:, 2, :])
+        turn_banks = ("bank3", "bank5", "bank3", "bank3")
+        back_banks = ("bank4", "bank6")
 
-        nc.vector.tensor_tensor(near[2][2][:], near[2][2][:], gate2_raw[:, 1:, :].rearrange("p d x -> p (d x)"), MULT)
-        nc.vector.tensor_tensor(third_last[:], third_last[:], gate2_raw[:, 2, :], MULT)
-        nc.vector.tensor_tensor(gate2_raw[:, 0, :], plain_first[:], gate2_raw[:, 0, :], MULT)
-        nc.vector.tensor_tensor(gate2_raw[:, 1, :], near[2][2][:, low], near[2][2][:, high], ADD)
-        nc.vector.tensor_tensor(result[:, 1, :], back_one[:], roots[1], ADD)
-        nc.sync.dma_start(out=out_rows[:, 1, :], in_=result[:, 1, :])
+        def sum_step_one(t, terms):
+            return turn_and_add(terms, V, 3.2, "turned_z%d" % t, turn_banks[t])
+
+        second_layer_tile(1, ("bank5", "bank6"))
+        centre = centre_term(0)
+        near = near_terms(0)
+        second_layer_tile(2, ("bank7", "bank0"))
+        next_centre = centre_term(1)
+        turned = sum_step_one(0, [near[0], centre] + near[1:])
+        second_layer_tile(3, ("bank1", "bank2"))
+
+        near = near_terms(1)
+        centre, next_centre = next_centre, centre_term(2)
+        root_term(0, "root0")
+        next_turned = sum_step_one(1, [centre] + near)
+        turn_back(turned, V, back_banks[0], z[0][:])
+
+        near = near_terms(2)
+        centre, next_centre = next_centre, centre_term(3)
+        plain_term(0, 0)
+        plain_term(0, 1)
+        turned, next_turned = next_turned, sum_step_one(2, [centre] + near)
+        turn_back(turned, V, back_banks[1], z[1][:])
+
+        near = near_terms(3)
+        plain_term(1, 0)
+        turn_back(next_turned, V, back_banks[0], z[2][:])
+        root_term(1, "turned_z2")
+        turned = sum_step_one(3, [next_centre] + near)
+        plain_term(2, 0)
+        turn_back(turned, V, back_banks[1], z[3][:])
+        root_term(2, "turned_z3")
+
+        result = keep.tile([P, PACK, U], F32, name="result", align_bytes=64)
+        far = keep.tile([P, last * D * U], F32, name="far", tag="near3_0", align_bytes=64)
+        gates_flat = gate2_raw[:].rearrange("p d x -> p (d x)")
+
+        def sum_step_two(t, tag):
+            first = t * D * U
+            n = PLAIN_TERMS[t]
+            if n:
+                nc.vector.tensor_tensor(far[:, first : first + n * U], plain[t][:], gates_flat[:, : n * U], MULT)
+            for d in range(n, D):
+                gated_gather(far[:, first + d * U : first + (d + 1) * U], z[t], nxt_t[d][:], gate2_raw[:, d, :])
+            terms = [roots[t][:]] + [far[:, first + d * U : first + (d + 1) * U] for d in range(D)]
+            if t:
+                terms = terms[1:] + terms[:1]
+            return turn_and_add(terms, U, 1.0, "turned_out%d" % t, tag)
+
+        def finish_tile(t, turned_sum, tag):
+            turn_back(turned_sum, U, tag, result[:, t, :])
+            nc.sync.dma_start(out=out_rows[:, t, :], in_=result[:, t, :])
+
+        sums = [sum_step_two(0, "bank7"), sum_step_two(1, "bank3")]
+        finish_tile(0, sums[0], "bank2")
+        root_term(3, "turned_out0")
+        sums.append(sum_step_two(2, "bank1"))
+        finish_tile(1, sums[1], "bank5")
+        finish_tile(2, sums[2], "bank4")
+
+        halves = [slice(0, U // 2), slice(U // 2, U)]
+        ends = [keep.tile([P, U], F32, name="end%d" % d, align_bytes=64) for d in range(D)]
         with_root = keep.tile([P, U], F32, align_bytes=64)
-        for cols in halves:
-            nc.vector.tensor_tensor(with_root[:, cols], root_first[:, cols], gate2_raw[:, 0, cols], ADD)
-        for cols in halves:
-            nc.vector.tensor_tensor(result[:, 0, cols], with_root[:, cols], gate2_raw[:, 1, cols], ADD)
-        nc.sync.dma_start(out=out_rows[:, 0, :], in_=result[:, 0, :])
-        for back, cols in zip(backs, halves):
-            nc.vector.tensor_tensor(result[:, last, cols], back[:], third_last[:, cols], ADD)
-        nc.sync.dma_start(out=out_rows[:, last, :], in_=result[:, last, :])
+        first_two = keep.tile([P, U], F32, align_bytes=64)
+        low, high = halves
 
+        def third_term(cols):
+            offsets = nxt_t[2][:, cols.start // 16 : cols.stop // 16]
+            gated_gather(ends[2][:, cols], z[last], offsets, gate2_raw[:, 2, cols])
+
+        for d in range(2):
+            gated_gather(ends[d][:], z[last], nxt_t[d][:], gate2_raw[:, d, :])
+        third_term(low)
+        nc.vector.tensor_tensor(first_two[:], ends[0][:], ends[1][:], ADD)
+        nc.vector.tensor_tensor(with_root[:, low], ends[2][:, low], roots[last][:, low], ADD)
+        nc.vector.tensor_tensor(with_root[:, high], first_two[:, high], roots[last][:, high], ADD)
+        third_term(high)
+        nc.vector.tensor_tensor(result[:, last, low], with_root[:, low], first_two[:, low], ADD)
+        nc.vector.tensor_tensor(result[:, last, high], with_root[:, high], ends[2][:, high], ADD)
+        nc.sync.dma_start(out=out_rows[:, last, :], in_=result[:, last, :])
         out_codes = keep.tile([P, U], U32, align_bytes=64)
         out_sc = keep.tile([P, U], U8, align_bytes=64)
         result_bf = [

@@ -370,21 +370,13 @@ def tile_picked_zappnp_none_po_kernel(
         ends = [keep.tile([P, U], F32, name="end%d" % d, align_bytes=64) for d in range(D)]
         with_root = keep.tile([P, U], F32, align_bytes=64)
         first_two = keep.tile([P, U], F32, align_bytes=64)
-        low, high = halves
-
-        def third_term(cols):
-            offsets = nxt_t[2][:, cols.start // 16 : cols.stop // 16]
-            gated_gather(ends[2][:, cols], z[last], offsets, gate2_raw[:, 2, cols])
-
-        for d in range(2):
+        for d in range(D):
             gated_gather(ends[d][:], z[last], nxt_t[d][:], gate2_raw[:, d, :])
-        third_term(low)
         nc.vector.tensor_tensor(first_two[:], ends[0][:], ends[1][:], ADD)
-        nc.vector.tensor_tensor(with_root[:, low], ends[2][:, low], roots[last][:, low], ADD)
-        nc.vector.tensor_tensor(with_root[:, high], first_two[:, high], roots[last][:, high], ADD)
-        third_term(high)
-        nc.vector.tensor_tensor(result[:, last, low], with_root[:, low], first_two[:, low], ADD)
-        nc.vector.tensor_tensor(result[:, last, high], with_root[:, high], ends[2][:, high], ADD)
+        for cols in halves:
+            nc.vector.tensor_tensor(with_root[:, cols], ends[2][:, cols], roots[last][:, cols], ADD)
+        for cols in halves:
+            nc.vector.tensor_tensor(result[:, last, cols], with_root[:, cols], first_two[:, cols], ADD)
         nc.sync.dma_start(out=out_rows[:, last, :], in_=result[:, last, :])
         out_codes = keep.tile([P, U], U32, align_bytes=64)
         out_sc = keep.tile([P, U], U8, align_bytes=64)
@@ -392,13 +384,18 @@ def tile_picked_zappnp_none_po_kernel(
             keep.tile([P, U // 2, PACK], BF16, name="result_bf", tag=tag, align_bytes=64)
             for tag in ("result_bf0", "result_bf1")
         ]
-        for u, cols in enumerate(halves):
-            dst = result_bf[u][:].rearrange("p (c i) t -> p c t i", i=4)
-            src = result[:, :, cols].rearrange("p t (c i) -> p c t i", i=4)
-            if u == 0:
-                nc.scalar.copy(out=dst, in_=src)
-            else:
-                nc.vector.tensor_copy(out=dst, in_=src)
+
+        def round_result(first, count, copy):
+            within = first % (U // 2)
+            dst = result_bf[first // (U // 2)][:, within : within + count, :]
+            copy(
+                out=dst.rearrange("p (c i) t -> p c t i", i=4),
+                in_=result[:, :, first : first + count].rearrange("p t (c i) -> p c t i", i=4),
+            )
+
+        round_result(0, U // 2, nc.vector.tensor_copy)
+        round_result(U // 2, U // 4, nc.scalar.copy)
+        round_result(3 * U // 4, U // 4, nc.vector.tensor_copy)
         for u, cols in enumerate(halves):
             nc.vector.quantize_mx(
                 out=out_codes[:, cols].bitcast(FP8X4),

from contextlib import ExitStack

import concourse.mybir as mybir
from concourse.masks import make_identity

K, T, S, D, V, H, N, U = 512, 4096, 1024, 3, 512, 512, 512, 256
FLOPS = 2 * K * H * S + 2 * H * N * S

F32 = mybir.dt.float32
BF16 = mybir.dt.bfloat16
I32 = mybir.dt.int32
U32 = mybir.dt.uint32
U16 = mybir.dt.uint16
U8 = mybir.dt.uint8
FP8X4 = mybir.dt.float8_e4m3fn_x4
MULT = mybir.AluOpType.mult
ADD = mybir.AluOpType.add
COPY = mybir.ActivationFunctionType.Copy

P = 128
PACK = 4
HALF = S // 2
CHUNK = 128
PIECES = ((0, 512), (512, 768), (768, 896), (896, 1024))
PIECE_ORDER = (0, 1, 2, 3)
VECTOR_CHUNKS = (2, 4)
Y_PIECES = PIECES
WARM = 2
SCALAR_ROWS = 48
LAST_SCALAR_ROWS = 32
FIRST_WORDS = 1280
PLAIN_TERMS = (2, 1, 1)


def tile_picked_zappnp_none_po_kernel(
    tc, x_words, x_scales, w1, w2_words, w2_scales, gate, gate2,
    offs, cen, pos1, pos2, pos3, nxt1, nxt2, nxt3, root, out_0, out_1, out_2,
):
    nc = tc.nc
    with ExitStack() as ctx:
        lists = ctx.enter_context(tc.tile_pool(name="lists", bufs=1))
        keep = ctx.enter_context(tc.tile_pool(name="keep", bufs=1))
        psum = ctx.enter_context(tc.psum_pool(name="psum", bufs=1))

        def load_list(name, source):
            tile = lists.tile(list(source.shape), U16, name=name)
            nc.sync.dma_start(tile[:], source)
            return tile

        def load_scale_rows(tile, source, queue):
            for r in range(4):
                queue.dma_start(
                    out=tile[r:P:32, :].bitcast(I32),
                    in_=source[0, r:16:4, :].bitcast(I32),
                )

        def load_w1(half, j0, j1):
            part = keep.tile([P, j1 - j0, H // 2], F32, name="w1_raw%d_%d" % (half, j0), align_bytes=64)
            nc.sync.dma_start(
                out=part[:],
                in_=w1.rearrange("(p j) c -> p j c", j=PACK)[:, j0:j1, half * H // 2 : (half + 1) * H // 2],
            )
            return part

        w2_scale_rows = keep.tile([P, N], U8, align_bytes=64)
        nc.vector.memset(w2_scale_rows[:].bitcast(I32), 0)
        x_scale_table = keep.tile([P, T], U8, tag="x_bytes", align_bytes=64)
        nc.vector.memset(x_scale_table[:].bitcast(I32), 0)
        x_word_table = keep.tile([P, T], U32, tag="x_table", align_bytes=64)
        x_word_rows = x_words[0].rearrange("p c r -> p (c r)").bitcast(I32)
        nc.sync.dma_start(out=x_word_table[:, :FIRST_WORDS].bitcast(I32), in_=x_word_rows[:, :FIRST_WORDS])
        offs_t = load_list("offs_t", offs)
        load_scale_rows(w2_scale_rows, w2_scales, nc.sync)
        nc.sync.dma_start(out=x_scale_table[4:P:8, :].bitcast(I32), in_=x_scales[0].bitcast(I32))
        nc.sync.dma_start(out=x_word_table[:, FIRST_WORDS:].bitcast(I32), in_=x_word_rows[:, FIRST_WORDS:])
        w1_raw = load_w1(0, 0, PACK)
        w1_late = [load_w1(1, j, j + 2) for j in (0, 2)]
        w2_raw = keep.tile([P, N], I32, tag="w2_raw", align_bytes=64)
        nc.sync.dma_start(out=w2_raw[:], in_=w2_words[0].rearrange("p c r -> p (c r)").bitcast(I32))
        pos_t = [load_list("pos%d_t" % d, src) for d, src in enumerate((pos1, pos2, pos3))]
        cen_t = load_list("cen_t", cen)
        gate_t = keep.tile([P, D, V], F32, align_bytes=64)
        nc.sync.dma_start(out=gate_t[:], in_=gate.rearrange("d p v -> p d v"))
        nxt_t = [load_list("nxt%d_t" % d, src) for d, src in enumerate((nxt1, nxt2, nxt3))]
        root_t = load_list("root_t", root)
        gate2_raw = keep.tile([P, D, U], F32, align_bytes=64)
        nc.sync.dma_start(out=gate2_raw[:], in_=gate2.rearrange("d p x -> p d x"))

        zero = keep.tile([P, 1], F32, align_bytes=64)
        nc.vector.memset(zero[:], 0.0)
        identity = keep.tile([P, P], F32, align_bytes=64)
        nc.scalar.activation(out=identity[:], in_=zero[:].to_broadcast([P, P]), func=COPY)
        make_identity(nc, identity[:], nomemset=True)

        w1_codes = keep.tile([P, H], U32, align_bytes=64)
        w1_sc = keep.tile([P, H], U8, align_bytes=64)

        def round_w1(half):
            dealt = [
                keep.tile([P, 2, P // 2, PACK], BF16, name="w1_bf", tag="w1_bf%d_%d" % (half, u), align_bytes=64)
                for u in range(2)
            ]
            dst = [tile[:].rearrange("p t m j -> p m t j") for tile in dealt]
            if half == 0:
                src = w1_raw[:].rearrange("p j (m t) -> p m t j", t=PACK)
                nc.scalar.activation(out=dst[1][:, :SCALAR_ROWS], in_=src[:, :SCALAR_ROWS, 2:, :], func=COPY)
                nc.vector.tensor_copy(out=dst[0], in_=src[:, :, :2, :])
                nc.vector.tensor_copy(out=dst[1][:, SCALAR_ROWS:], in_=src[:, SCALAR_ROWS:, 2:, :])
                return dealt
            for pair, part in enumerate(w1_late):
                src = part[:].rearrange("p j (m t) -> p m t j", t=PACK)
                rows = slice(2 * pair, 2 * pair + 2)
                split = LAST_SCALAR_ROWS if pair else P // 2
                nc.scalar.activation(out=dst[1][:, :split, :, rows], in_=src[:, :split, 2:, :], func=COPY)
                nc.vector.tensor_copy(out=dst[0][:, :, :, rows], in_=src[:, :, :2, :])
                if pair:
                    nc.vector.tensor_copy(out=dst[1][:, split:, :, rows], in_=src[:, split:, 2:, :])
            return dealt

        def quantise_w1(half, u, dealt):
            for i in range(2):
                first = (2 * u + i) * P + half * P // 2
                cols = slice(first, first + P // 2)
                nc.vector.quantize_mx(
                    out=w1_codes[:, cols].bitcast(FP8X4),
                    scales=w1_sc[:, cols],
                    in_=dealt[:, i, :, :].rearrange("p m j -> p (m j)"),
                )

        def gather_words(u, tag):
            codes = keep.tile([P, HALF], U32, name="x_codes", tag=tag, align_bytes=64)
            nc.vector.tensor_copy(
                codes[:], x_word_table[:].indirect(offs_t[:, u * HALF // 16 : (u + 1) * HALF // 16])
            )
            return codes

        x_sc_spread = keep.tile([P, S], U8, align_bytes=64)
        nc.vector.tensor_copy(x_sc_spread[:], x_scale_table[:].indirect(offs_t[:]))
        x_sc = keep.tile([P, S], U8, align_bytes=64)
        nc.vector.memset(x_sc[:].bitcast(I32), 0)
        for r in range(4):
            nc.scalar.dma_start(
                out=x_sc[r:P:32, :].bitcast(I32), in_=x_sc_spread[8 * r + 4 : P : 32, :].bitcast(I32)
            )
        w2_sc_dealt = keep.tile([P, PACK, P], U8, align_bytes=64)
        nc.vector.tensor_copy(
            out=w2_sc_dealt[:].rearrange("p t m -> p m t"),
            in_=w2_scale_rows[:].rearrange("p (m t) -> p m t", t=PACK),
        )
        w2_sc = [w2_sc_dealt[:, t, :] for t in range(PACK)]
        x_codes = [gather_words(0, "x_bytes")]
        for t in range(WARM):
            warm = psum.tile([P, HALF], F32, name="warm", tag="bank%d" % (4 + t))
            nc.tensor.matmul_mx(
                out=warm[:],
                lhsT=x_codes[0][:, t * P : (t + 1) * P].bitcast(FP8X4),
                lhsT_scale=w2_sc[t],
                rhs=x_codes[0][:].bitcast(FP8X4),
                rhs_scale=w2_sc_dealt[:].rearrange("p t m -> p (t m)"),
                start=True,
                stop=True,
            )
        for half in range(2):
            late = round_w1(half)
            for u in range(2):
                quantise_w1(half, u, late[u])
        x_codes.append(gather_words(1, "w1_raw1_2"))

        h_codes = keep.tile([P, S], U32, align_bytes=64)
        h_sc = keep.tile([P, S], U8, align_bytes=64)
        y = [keep.tile([P, S], F32, name="y%d" % t, align_bytes=64) for t in range(PACK)]
        h_bf = [
            keep.tile([P, b - a, PACK], BF16, name="h_bf", tag="h_bf%d" % i, align_bytes=64)
            for i, (a, b) in enumerate(PIECES)
        ]

        def first_layer(first, width, tag):
            bank = psum.tile([P, PACK, width], F32, name="h_bank", tag=tag)
            for t in range(PACK) if first == 0 else reversed(range(PACK)):
                nc.tensor.matmul_mx(
                    out=bank[:, t, :],
                    lhsT=w1_codes[:, t * P : (t + 1) * P].bitcast(FP8X4),
                    lhsT_scale=w1_sc[:, t * P : (t + 1) * P],
                    rhs=x_codes[first // HALF][:, first % HALF : first % HALF + width].bitcast(FP8X4),
                    rhs_scale=x_sc[:, first : first + width],
                    start=True,
                    stop=True,
                )
            return bank

        def round_hidden(bank, first, width, on_vector):
            piece = max(i for i, (a, b) in enumerate(PIECES) if a <= first)
            within = first - PIECES[piece][0]
            dst = h_bf[piece][:, within : within + width, :]
            src = bank[:].rearrange("p t n -> p n t")
            if on_vector:
                nc.vector.tensor_copy(out=dst, in_=src)
            else:
                nc.scalar.copy(out=dst, in_=src)

        def quantise_hidden(piece):
            cols = slice(*PIECES[piece])
            nc.vector.quantize_mx(
                out=h_codes[:, cols].bitcast(FP8X4),
                scales=h_sc[:, cols],
                in_=h_bf[piece][:].rearrange("p n t -> p (n t)"),
            )

        def second_layer(t, cols, on_vector, tag):
            bank = psum.tile([P, cols.stop - cols.start], F32, name="y_bank", tag=tag)
            nc.tensor.matmul_mx(
                out=bank[:],
                lhsT=w2_codes[t].bitcast(FP8X4),
                lhsT_scale=w2_sc[t],
                rhs=h_codes[:, cols].bitcast(FP8X4),
                rhs_scale=h_sc[:, cols],
                start=True,
                stop=True,
            )
            if on_vector:
                nc.vector.tensor_scalar_mul(y[t][:, cols], bank[:], 0.2)
            else:
                nc.scalar.activation(out=y[t][:, cols], in_=bank[:], func=COPY, scale=0.2)

        for chunk in range(S // CHUNK - 1):
            first = chunk * CHUNK
            bank = first_layer(first, CHUNK, "bank%d" % chunk)
            round_hidden(bank, first, CHUNK, chunk in VECTOR_CHUNKS)
        tail_bank = first_layer(S - CHUNK // 2, CHUNK // 2, "bank7")
        round_hidden(first_layer(S - CHUNK, CHUNK // 2, "bank0"), S - CHUNK, CHUNK // 2, False)

        w2_word_view = w2_raw[:].rearrange("p (m t) -> p m t", t=PACK)
        w2_codes_first = keep.tile([P, P], I32, tag="w1_bf1_1", align_bytes=64)
        nc.vector.tensor_copy(out=w2_codes_first[:], in_=w2_word_view[:, :, 0])
        w2_codes = [w2_codes_first[:]]

        quantise_hidden(0)
        round_hidden(tail_bank, S - CHUNK // 2, CHUNK // 2, True)
        for piece in PIECE_ORDER[1:]:
            quantise_hidden(piece)
        for i, (a, b) in enumerate(Y_PIECES):
            second_layer(0, slice(a, b), a == 512, "bank%d" % (1 + i))
        last_piece = "h_bf%d" % PIECE_ORDER[-1]
        w2_codes_rest = keep.tile([P, PACK - 1, P], I32, tag=last_piece, align_bytes=64)
        nc.vector.tensor_copy(out=w2_codes_rest[:].rearrange("p t m -> p m t"), in_=w2_word_view[:, :, 1:])
        w2_codes.extend(w2_codes_rest[:, t, :] for t in range(PACK - 1))

        def second_layer_tile(t, banks):
            for u in range(2):
                second_layer(t, slice(u * HALF, (u + 1) * HALF), False, banks[u])

        def turn_and_add(terms, width, scale, name, tag):
            blocks = [slice(b * P, (b + 1) * P) for b in range(width // P)]
            turned = psum.tile([P, width], F32, name="turned", tag=tag)
            for i, term in enumerate(terms):
                for b, cols in enumerate(blocks):
                    nc.tensor.matmul(
                        turned[:, cols], term[:, cols], identity[:],
                        start=(i == 0 and b == 0),
                        stop=(i == len(terms) - 1 and b == len(blocks) - 1),
                        is_transpose=True,
                    )
            turned_sb = keep.tile([P, width], F32, name="turned_sb", tag=name, align_bytes=64)
            nc.scalar.activation(out=turned_sb[:], in_=turned[:], func=COPY, scale=scale)
            return turned_sb

        def turn_back(turned_sb, width, tag, dst):
            back = psum.tile([P, width], F32, name="back", tag=tag)
            for b in range(width // P):
                cols = slice(b * P, (b + 1) * P)
                nc.tensor.transpose(back[:, cols], turned_sb[:, cols], identity[:])
            nc.scalar.copy(out=dst, in_=back[:])

        def gated_gather(dst, window, offsets, gates):
            nc.vector.tensor_tensor(dst, window[:].indirect(offsets), gates, MULT)

        def plain_gather(dst, window, offsets):
            nc.scalar.activation(out=dst, in_=window[:].indirect(offsets), func=COPY)

        def centre_term(t):
            own = keep.tile([P, V], F32, name="own%d" % t, align_bytes=64)
            nc.scalar.activation(out=own[:], in_=y[t][:].indirect(cen_t[:]), func=COPY, scale=0.25)
            return own[:]

        def near_terms(t):
            terms = []
            for d in range(D):
                term = keep.tile([P, V], F32, name="near", tag="near%d_%d" % (t, d), align_bytes=64)
                gated_gather(term[:], y[t], pos_t[d][:], gate_t[:, d, :])
                terms.append(term[:])
            return terms

        last = PACK - 1
        z = [keep.tile([P, V], F32, name="z%d" % t, align_bytes=64) for t in range(PACK)]
        roots = []
        plain = [keep.tile([P, n * U], F32, name="plain%d" % t, align_bytes=64) for t, n in enumerate(PLAIN_TERMS) if n]
        out_rows = out_0.rearrange("(p t) x -> p t x", t=PACK)

        def plain_term(t, d):
            plain_gather(plain[t][:, d * U : (d + 1) * U], z[t], nxt_t[d][:])

        def root_term(t, tag):
            roots.append(keep.tile([P, U], F32, name="root", tag=tag, align_bytes=64))
            plain_gather(roots[t][:], y[t], root_t[:])

        turn_banks = ("bank3", "bank5", "bank3", "bank3")
        back_banks = ("bank4", "bank6")

        def sum_step_one(t, terms):
            return turn_and_add(terms, V, 3.2, "turned_z%d" % t, turn_banks[t])

        second_layer_tile(1, ("bank5", "bank6"))
        centre = centre_term(0)
        near = near_terms(0)
        second_layer_tile(2, ("bank7", "bank0"))
        next_centre = centre_term(1)
        turned = sum_step_one(0, [near[0], centre] + near[1:])
        second_layer_tile(3, ("bank1", "bank2"))

        near = near_terms(1)
        centre, next_centre = next_centre, centre_term(2)
        root_term(0, "root0")
        next_turned = sum_step_one(1, [centre] + near)
        turn_back(turned, V, back_banks[0], z[0][:])

        near = near_terms(2)
        centre, next_centre = next_centre, centre_term(3)
        plain_term(0, 0)
        plain_term(0, 1)
        turned, next_turned = next_turned, sum_step_one(2, [centre] + near)
        turn_back(turned, V, back_banks[1], z[1][:])

        near = near_terms(3)
        plain_term(1, 0)
        turn_back(next_turned, V, back_banks[0], z[2][:])
        root_term(1, "turned_z2")
        turned = sum_step_one(3, [next_centre] + near)
        plain_term(2, 0)
        turn_back(turned, V, back_banks[1], z[3][:])
        root_term(2, "turned_z3")

        result = keep.tile([P, PACK, U], F32, name="result", align_bytes=64)
        far = keep.tile([P, last * D * U], F32, name="far", tag="near3_0", align_bytes=64)
        gates_flat = gate2_raw[:].rearrange("p d x -> p (d x)")

        def sum_step_two(t, tag):
            first = t * D * U
            n = PLAIN_TERMS[t]
            if n:
                nc.vector.tensor_tensor(far[:, first : first + n * U], plain[t][:], gates_flat[:, : n * U], MULT)
            for d in range(n, D):
                gated_gather(far[:, first + d * U : first + (d + 1) * U], z[t], nxt_t[d][:], gate2_raw[:, d, :])
            terms = [roots[t][:]] + [far[:, first + d * U : first + (d + 1) * U] for d in range(D)]
            if t:
                terms = terms[1:] + terms[:1]
            return turn_and_add(terms, U, 1.0, "turned_out%d" % t, tag)

        def finish_tile(t, turned_sum, tag):
            turn_back(turned_sum, U, tag, result[:, t, :])
            nc.sync.dma_start(out=out_rows[:, t, :], in_=result[:, t, :])

        sums = [sum_step_two(0, "bank7"), sum_step_two(1, "bank3")]
        finish_tile(0, sums[0], "bank2")
        root_term(3, "turned_out0")
        sums.append(sum_step_two(2, "bank1"))
        finish_tile(1, sums[1], "bank5")
        finish_tile(2, sums[2], "bank4")

        halves = [slice(0, U // 2), slice(U // 2, U)]
        ends = [keep.tile([P, U], F32, name="end%d" % d, align_bytes=64) for d in range(D)]
        with_root = keep.tile([P, U], F32, align_bytes=64)
        first_two = keep.tile([P, U], F32, align_bytes=64)
        for d in range(D):
            gated_gather(ends[d][:], z[last], nxt_t[d][:], gate2_raw[:, d, :])
        nc.vector.tensor_tensor(first_two[:], ends[0][:], ends[1][:], ADD)
        for cols in halves:
            nc.vector.tensor_tensor(with_root[:, cols], ends[2][:, cols], roots[last][:, cols], ADD)
        for cols in halves:
            nc.vector.tensor_tensor(result[:, last, cols], with_root[:, cols], first_two[:, cols], ADD)
        nc.sync.dma_start(out=out_rows[:, last, :], in_=result[:, last, :])
        out_codes = keep.tile([P, U], U32, align_bytes=64)
        out_sc = keep.tile([P, U], U8, align_bytes=64)
        result_bf = [
            keep.tile([P, U // 2, PACK], BF16, name="result_bf", tag=tag, align_bytes=64)
            for tag in ("result_bf0", "result_bf1")
        ]

        def round_result(first, count, copy):
            within = first % (U // 2)
            dst = result_bf[first // (U // 2)][:, within : within + count, :]
            copy(
                out=dst.rearrange("p (c i) t -> p c t i", i=4),
                in_=result[:, :, first : first + count].rearrange("p t (c i) -> p c t i", i=4),
            )

        round_result(0, U // 2, nc.vector.tensor_copy)
        round_result(U // 2, U // 4, nc.scalar.copy)
        round_result(3 * U // 4, U // 4, nc.vector.tensor_copy)
        for u, cols in enumerate(halves):
            nc.vector.quantize_mx(
                out=out_codes[:, cols].bitcast(FP8X4),
                scales=out_sc[:, cols],
                in_=result_bf[u][:].rearrange("p x t -> p (x t)"),
            )
        nc.sync.dma_start(
            out=out_1[0].rearrange("p c r -> p (c r)").bitcast(I32),
            in_=out_codes[:].bitcast(I32),
        )
        for q in range(4):
            queue = nc.scalar if q % 2 == 0 else nc.sync
            queue.dma_start(
                out=out_2[0, 4 * q : 4 * q + 4, :].bitcast(I32),
                in_=out_sc[32 * q : 32 * q + 4, :].bitcast(I32),
            )
